import numpy as np
import ml_dtypes


def mxq(x, axis, fmt="e4m3"):
    dtype, down = {"e4m3": (ml_dtypes.float8_e4m3fn, 7), "e5m2": (ml_dtypes.float8_e5m2, 14)}[fmt]
    v = np.moveaxis(np.asarray(x, np.float32).astype(ml_dtypes.bfloat16).astype(np.float64), axis, -1)
    blocks = v.reshape(v.shape[:-1] + (-1, 32))
    amax = np.abs(blocks).max(-1, keepdims=True)
    byte = np.maximum(np.where(amax > 0, np.frexp(amax)[1] - 1 + 127, 0) - down, 1)
    scale = np.exp2(byte - 127.0)
    codes = (blocks / scale).astype(np.float32).astype(dtype).astype(np.float64)
    return np.moveaxis((codes * scale).reshape(v.shape), -1, axis)


WIDE = False


def mx_kscale(k):
    if not WIDE:
        return np.ones(k)
    levels = np.array([10, -10, 5, -5, 0])
    if k % 512:
        return np.exp2(np.random.permutation(np.resize(levels, k // 32))).repeat(32)
    a = np.empty((k // 512, 16))
    for p in range(k // 512):
        a[p, :8] = np.random.permutation(np.resize(levels, 8))
        for g in range(8):
            far = levels[np.abs(levels - a[p, g]) >= 10]
            a[p, g + 8] = far[np.random.randint(len(far))]
    return np.exp2(a.ravel()).repeat(32)


def f64(x):
    return np.asarray(x).astype(np.float64)


def striped(idx):
    return np.tile(idx.reshape(-1, 16).T, (8, 1)).astype(np.uint16)


def unstriped(offs):
    return offs[:16].T.reshape(-1).astype(np.int64)


E2M1 = np.array([0.0, 0.5, 1.0, 1.5, 2.0, 3.0, 4.0, 6.0, -0.0, -0.5, -1.0, -1.5, -2.0, -3.0, -4.0, -6.0])


def pack_weight(w, fmt):
    k, n = w.shape
    w = f64(np.asarray(w, np.float32).astype(ml_dtypes.bfloat16)).reshape(k // 32, 32, n)
    amax = np.abs(w).max(1)
    if fmt == "e4m3":
        byte = np.frexp(amax)[1] - 1 + 127 - 7
    else:
        mant, ex = np.frexp(amax / 6.0)
        byte = np.where(mant > 0.5, ex, ex - 1) + 127
    byte = np.clip(np.where(amax > 0, byte, 1), 1, 254)
    scaled = (w * np.exp2(127.0 - byte)[:, None, :]).reshape(k, n).astype(np.float32)
    by_word = np.ascontiguousarray(scaled.reshape(k // 512, 128, 4, n).transpose(0, 1, 3, 2))
    if fmt == "e4m3":
        words = by_word.astype(ml_dtypes.float8_e4m3fn).view(np.uint8)
    else:
        c = by_word.astype(ml_dtypes.float4_e2m1fn).view(np.uint8) & 0xF
        words = (c[..., 0::2] | (c[..., 1::2] << 4)).reshape(k // 512, 128, 2 * n)
    return np.ascontiguousarray(words), np.ascontiguousarray(byte.astype(np.uint8).reshape(k // 512, 16, n))


def unpack_weight(words, scales, fmt):
    g, _, n = scales.shape
    words = np.ascontiguousarray(words).reshape(g, 128, n, -1)
    if fmt == "e4m3":
        vals = words.view(ml_dtypes.float8_e4m3fn).astype(np.float64)
    else:
        nib = np.empty((g, 128, n, 4), np.uint8)
        nib[..., 0::2] = words & 0xF
        nib[..., 1::2] = words >> 4
        vals = E2M1[nib]
    vals = vals * np.repeat(np.exp2(scales.astype(np.float64) - 127.0), 8, axis=1)[..., None]
    return vals.transpose(0, 1, 3, 2).reshape(g * 512, n)


def gelu(v):
    return 0.5 * v * (1.0 + np.tanh(np.sqrt(2.0 / np.pi) * (v + 0.044715 * v**3)))


K, H, T, S, P = 1024, 1024, 4096, 1024, 512

def setup_inputs():
    n = np.random.standard_normal
    s = mx_kscale(K)[:, None]
    u = mx_kscale(H)[:, None]
    tab_words, tab_scales = pack_weight(n((K, T)) * s, "e4m3")
    w2_words, w2_scales = pack_weight(n((H, H)) / np.sqrt(H) / u, "e2m1")
    w3_words, w3_scales = pack_weight(n((H, H)) / np.sqrt(H) / u, "e4m3")
    return {
        "tab_words": tab_words, "tab_scales": tab_scales,
        "offs": striped(np.random.permutation(T)[:S]),
        "pos1": striped(np.random.permutation(S)[:P]),
        "pos2": striped(np.random.permutation(S)[:P]),
        "w1": (n((K, H)) / np.sqrt(K) / s * u.T).astype(np.float32),
        "w2_words": w2_words, "w2_scales": w2_scales,
        "w3_words": w3_words, "w3_scales": w3_scales,
        "tone": (np.exp(0.3 * n(H)) / u[:, 0]).astype(np.float32),
        "gain": (np.exp(0.3 * n(H)) * u[:, 0]).astype(np.float32),
        "skip": (np.exp(0.3 * n(H)) / u[:, 0]).astype(np.float32),
    }

def reference(tab_words, tab_scales, offs, pos1, pos2, w1, w2_words, w2_scales,
              w3_words, w3_scales, tone, gain, skip):
    v = unpack_weight(tab_words, tab_scales, "e4m3")[:, unstriped(offs)]
    w2 = unpack_weight(w2_words, w2_scales, "e2m1")
    w3 = unpack_weight(w3_words, w3_scales, "e4m3")
    h = mxq(f64(w1), 0, "e4m3").T @ v
    d = h[:, unstriped(pos1)] * f64(tone)[:, None]
    x = 0.5 * d * (1 + np.tanh(np.sqrt(2 / np.pi) * (d + 0.044715 * d ** 3)))
    x = x * f64(gain)[:, None]
    b = h[:, unstriped(pos2)]
    y = w2.T @ mxq(x, 0, "e4m3") + w3.T @ mxq(b, 0, "e4m3")
    return np.tanh(y) + b * f64(skip)[:, None]

@@ -1,0 +1,321 @@
+from contextlib import ExitStack
+
+import concourse.mybir as mybir
+from concourse.masks import make_identity
+
+K, H, T, S, M = 1024, 1024, 4096, 1024, 512
+FLOPS = 2 * K * H * S + 2 * 2 * H * H * M
+
+F32 = mybir.dt.float32
+BF16 = mybir.dt.bfloat16
+I32 = mybir.dt.int32
+U32 = mybir.dt.uint32
+U16 = mybir.dt.uint16
+U8 = mybir.dt.uint8
+FP8X4 = mybir.dt.float8_e4m3fn_x4
+FP4X4 = mybir.dt.float4_e2m1fn_x4
+ACT = mybir.ActivationFunctionType
+ALU = mybir.AluOpType
+
+P = 128
+PACK = 4
+PASS = P * PACK
+BANK = 512
+LIST_ROWS = 16
+CHUNKS = ((0, 256), (256, 256))
+VECTOR_SHARE = 88
+
+
+def tile_list_citation_chain_reader_kernel(
+    tc, tab_words, tab_scales, offs, pos1, pos2, w1, w2_words, w2_scales,
+    w3_words, w3_scales, tone, gain, skip, out,
+):
+    nc = tc.nc
+    with ExitStack() as ctx:
+        lists = ctx.enter_context(tc.tile_pool(name="lists", bufs=1))
+        keep = ctx.enter_context(tc.tile_pool(name="keep", bufs=1))
+        psum = ctx.enter_context(tc.psum_pool(name="psum", bufs=1))
+
+        def bank(number, shape):
+            return psum.tile(shape, F32, name="bank", tag="bank%d" % number)
+
+        offs_sb = lists.tile([P, S // LIST_ROWS], U16)
+        pos1_sb = lists.tile([P, M // LIST_ROWS], U16)
+        pos2_sb = lists.tile([P, M // LIST_ROWS], U16)
+
+        tab_sc = keep.tile([P, T], U8, align_bytes=64)
+        w2_sc = keep.tile([P, 2 * H], U8, align_bytes=64)
+        w3_sc = keep.tile([P, 2 * H], U8, align_bytes=64)
+        nc.vector.memset(tab_sc[:].bitcast(I32), 0)
+        nc.vector.memset(w2_sc[:].bitcast(I32), 0)
+        nc.vector.memset(w3_sc[:].bitcast(I32), 0)
+
+        warm = keep.tile([P, 8], F32)
+        nc.vector.memset(warm[:], 0.0)
+        nc.scalar.activation(warm[:], warm[:], ACT.Gelu_apprx_tanh)
+
+        tab_w = [keep.tile([P, T], I32, name="tab_w%d" % g, align_bytes=64) for g in range(2)]
+        w1_raw = {}
+
+        def load_table(g):
+            nc.sync.dma_start(tab_w[g][:], tab_words[g].rearrange("p n i -> p (n i)").bitcast(I32))
+
+        def load_w1(a, g):
+            raw = keep.tile([P, PACK, PASS], F32, name="w1_raw%d%d" % (a, g))
+            rows = w1[g * PASS : (g + 1) * PASS, a * PASS : (a + 1) * PASS]
+            nc.sync.dma_start(raw[:], rows.rearrange("(p j) c -> p j c", j=PACK))
+            w1_raw[a, g] = raw
+
+        tone_sb = keep.tile([P, 2, PACK], F32)
+        gain_sb = keep.tile([P, 2, PACK], F32)
+        skip_sb = keep.tile([P, 2, PACK], F32)
+
+        def load_factor(dst, vec):
+            nc.sync.dma_start(dst[:], vec.rearrange("(a p t) -> p a t", a=2, t=PACK))
+
+        load_table(0)
+        nc.sync.dma_start(offs_sb[:], offs)
+        load_w1(0, 0)
+        load_table(1)
+        load_w1(0, 1)
+        nc.sync.dma_start(pos1_sb[:], pos1)
+        nc.sync.dma_start(pos2_sb[:], pos2)
+        load_factor(tone_sb, tone)
+        load_w1(1, 0)
+        load_factor(gain_sb, gain)
+        load_w1(1, 1)
+        load_factor(skip_sb, skip)
+        w3_w = keep.tile([P, 2, H], I32, align_bytes=64)
+        nc.sync.dma_start(w3_w[:], w3_words.rearrange("a p n i -> p a (n i)").bitcast(I32))
+        w2_w = keep.tile([P, 2, 2 * H], U8, align_bytes=64)
+        nc.sync.dma_start(w2_w[:].bitcast(I32), w2_words.rearrange("a p n -> p a n").bitcast(I32))
+        for plane, rows in ((w3_sc, w3_scales), (w2_sc, w2_scales)):
+            for q in range(4):
+                nc.sync.dma_start(
+                    plane[32 * q : 32 * q + 4, :].bitcast(I32).rearrange("r (a n) -> r a n", a=2),
+                    rows[:, 4 * q : 4 * q + 4, :].rearrange("a r n -> r a n").bitcast(I32),
+                )
+
+        for q in range(4):
+            nc.gpsimd.dma_start(
+                tab_sc[32 * q : 32 * q + 8, :].bitcast(I32),
+                tab_scales[:, 4 * q : 4 * q + 4, :].bitcast(I32),
+            )
+        ident = keep.tile([P, P], F32)
+        make_identity(nc, ident[:])
+
+        v_w = [keep.tile([P, S], U32, name="v_w%d" % g, align_bytes=64) for g in range(2)]
+        v_sc = keep.tile([P, S], U8, align_bytes=64)
+
+        def gather_table(g):
+            nc.vector.tensor_copy(v_w[g][:], tab_w[g][:].bitcast(U32).indirect(offs_sb[:]))
+
+        w1_bf, w1_q = {}, {}
+
+        def round_w1(a, g, vector_share):
+            grouped = keep.tile([P, PASS * PACK], BF16, name="w1_bf", tag="w1_bf", bufs=2, align_bytes=64)
+            dst = grouped[:].rearrange("p (t m j) -> p m j t", t=PACK, j=PACK)
+            src = w1_raw[a, g][:].rearrange("p j (m t) -> p m j t", t=PACK)
+            if vector_share > 0:
+                nc.vector.tensor_copy(dst[:, :vector_share], src[:, :vector_share])
+            if vector_share < P:
+                nc.scalar.copy(dst[:, vector_share:], src[:, vector_share:])
+            w1_bf[a, g] = grouped
+
+        def quantise(name, values, widths):
+            words = values.shape[1] // PACK
+            codes = keep.tile([P, words], U32, name=name + "_codes", align_bytes=64)
+            scales = keep.tile([P, words], U8, name=name + "_scales", align_bytes=64)
+            c0 = 0
+            for width in widths:
+                nc.vector.quantize_mx(
+                    out=codes[:, c0 : c0 + width].bitcast(FP8X4),
+                    scales=scales[:, c0 : c0 + width],
+                    in_=values[:, PACK * c0 : PACK * (c0 + width)],
+                )
+                c0 += width
+            return codes, scales
+
+        def quantise_w1(a, g, widths):
+            w1_q[a, g] = quantise("w1_%d%d" % (a, g), w1_bf[a, g], widths)
+
+        h_acc, h = {}, {}
+
+        def first_stage_pass(a, t, g):
+            codes, scales = w1_q[a, g]
+            for half in range(2):
+                if g == 0:
+                    h_acc[a, t, half] = bank(2 * t + half, [P, BANK])
+                cols = slice(half * BANK, (half + 1) * BANK)
+                nc.tensor.matmul_mx(
+                    out=h_acc[a, t, half][:],
+                    lhsT=codes[:, t * P : (t + 1) * P].bitcast(FP8X4),
+                    lhsT_scale=scales[:, t * P : (t + 1) * P],
+                    rhs=v_w[g][:, cols].bitcast(FP8X4),
+                    rhs_scale=v_sc[4 * g : P, cols],
+                    start=(g == 0),
+                    stop=(g == 1),
+                )
+
+        def fetch_h(a, t, vector_helps=False):
+            rows = keep.tile([P, S], F32, name="h%d%d" % (a, t))
+            nc.scalar.copy(rows[:, :BANK], h_acc[a, t, 0][:])
+            if vector_helps:
+                nc.vector.tensor_copy(rows[:, BANK:], h_acc[a, t, 1][:])
+            else:
+                nc.scalar.copy(rows[:, BANK:], h_acc[a, t, 1][:])
+            h[a, t] = rows
+
+        quoted, rebut, x_q, b_q = {}, {}, {}, {}
+
+        def open_piece(a, m0, mc):
+            quoted[a, m0] = keep.tile([P, PACK, mc], F32, name="quoted%d_%d" % (a, m0))
+            rebut[a, m0] = keep.tile([P, PACK, mc], F32, name="rebut%d_%d" % (a, m0))
+
+        def gather_quoted(a, m0, mc, t):
+            picks = pos1_sb[:, m0 // LIST_ROWS : (m0 + mc) // LIST_ROWS]
+            d = quoted[a, m0][:, t, :]
+            nc.vector.tensor_copy(d, h[a, t][:].indirect(picks))
+            nc.scalar.activation(d, d, ACT.Gelu_apprx_tanh, scale=tone_sb[:, a, t : t + 1])
+
+        def gather_rebut(a, m0, mc, t):
+            picks = pos2_sb[:, m0 // LIST_ROWS : (m0 + mc) // LIST_ROWS]
+            nc.vector.tensor_copy(rebut[a, m0][:, t, :], h[a, t][:].indirect(picks))
+
+        x_bf, b_bf = {}, {}
+
+        def woven(tile, mc):
+            return tile[:].rearrange("p (c i t) -> p c t i", i=4, t=PACK)
+
+        def planes(tile):
+            return tile[:].rearrange("p t (c i) -> p c t i", i=4)
+
+        def round_x(a, m0, mc):
+            values = keep.tile([P, mc * PACK], BF16, name="x_bf%d_%d" % (a, m0), align_bytes=64)
+            factor = gain_sb[:, a, :].unsqueeze(1).unsqueeze(3).to_broadcast([P, mc // 4, PACK, 4])
+            nc.vector.tensor_tensor(woven(values, mc), planes(quoted[a, m0]), factor, ALU.mult)
+            x_bf[a, m0] = values
+
+        def round_b(a, m0, mc):
+            values = keep.tile([P, mc * PACK], BF16, name="b_bf%d_%d" % (a, m0), align_bytes=64)
+            nc.scalar.copy(woven(values, mc), planes(rebut[a, m0]))
+            b_bf[a, m0] = values
+
+        def quantise_x(a, m0, mc):
+            x_q[a, m0] = quantise("x%d_%d" % (a, m0), x_bf[a, m0], [mc])
+
+        def quantise_b(a, m0, mc):
+            b_q[a, m0] = quantise("b%d_%d" % (a, m0), b_bf[a, m0], [mc])
+
+        y_acc = {}
+
+        def second_stage_passes(a, piece_m0, mt):
+            c0 = mt * P - piece_m0
+            for half in range(2):
+                if a == 0:
+                    y_acc[mt, half] = bank(2 * mt + half, [P, BANK])
+                n0 = half * BANK
+                codes, scales = b_q[a, piece_m0]
+                nc.tensor.matmul_mx(
+                    out=y_acc[mt, half][:],
+                    lhsT=codes[:, c0 : c0 + P].bitcast(FP8X4),
+                    lhsT_scale=scales[:, c0 : c0 + P],
+                    rhs=w3_w[:, a, n0 : n0 + BANK].bitcast(FP8X4),
+                    rhs_scale=w3_sc[:, a * H + n0 : a * H + n0 + BANK],
+                    start=(a == 0),
+                    stop=False,
+                )
+                codes, scales = x_q[a, piece_m0]
+                nc.tensor.matmul_mx(
+                    out=y_acc[mt, half][:],
+                    lhsT=codes[:, c0 : c0 + P].bitcast(FP8X4),
+                    lhsT_scale=scales[:, c0 : c0 + P],
+                    rhs=w2_w[:, a, 2 * n0 : 2 * (n0 + BANK)].bitcast(FP4X4),
+                    rhs_scale=w2_sc[:, a * H + n0 : a * H + n0 + BANK],
+                    start=False,
+                    stop=(a == 1),
+                )
+
+        def finish(m0, mc, half):
+            tiles = range(m0 // P, (m0 + mc) // P)
+            bent = {}
+            for mt in tiles:
+                bent[mt] = keep.tile([P, PACK, P], F32, name="bent", tag="bent", bufs=4)
+                nc.scalar.activation(
+                    bent[mt][:], y_acc[mt, half][:].rearrange("m (p t) -> m t p", t=PACK), ACT.Tanh
+                )
+            per_bank = PACK // len(tiles)
+            result = keep.tile([P, PACK, mc], F32, name="result%d_%d" % (half, m0))
+            piece_m0 = 0 if half == 0 else m0
+            c0 = m0 - piece_m0
+            for number, mt_bank in enumerate(tiles):
+                turned = bank(2 * mt_bank + half, [P, per_bank, mc])
+                for u in range(per_bank):
+                    t = number * per_bank + u
+                    for mt in tiles:
+                        nc.tensor.transpose(turned[:, u, mt * P - m0 : (mt + 1) * P - m0], bent[mt][:, t, :], ident[:])
+                for u in range(per_bank):
+                    t = number * per_bank + u
+                    nc.vector.scalar_tensor_tensor(
+                        result[:, t, :], rebut[half, piece_m0][:, t, c0 : c0 + mc], skip_sb[:, half, t : t + 1],
+                        turned[:, u, :], ALU.mult, ALU.add,
+                    )
+            rows = out[half * PASS : (half + 1) * PASS, m0 : m0 + mc]
+            nc.sync.dma_start(rows.rearrange("(p t) m -> p t m", t=PACK), result[:])
+
+        gather_table(0)
+        nc.vector.tensor_copy(v_sc[:], tab_sc[:].indirect(offs_sb[:]))
+        round_w1(0, 0, P)
+        quantise_w1(0, 0, [PASS])
+        for t in range(PACK):
+            first_stage_pass(0, t, 0)
+        gather_table(1)
+        round_w1(0, 1, VECTOR_SHARE)
+        quantise_w1(0, 1, [P] * PACK)
+        for t in range(PACK):
+            first_stage_pass(0, t, 1)
+        open_piece(0, 0, M)
+        fetch_h(0, 0, vector_helps=True)
+        fetch_h(0, 1)
+        gather_quoted(0, 0, M, 0)
+        gather_rebut(0, 0, M, 0)
+        fetch_h(0, 2)
+        gather_quoted(0, 0, M, 1)
+        fetch_h(0, 3)
+        round_w1(1, 0, 0)
+        gather_rebut(0, 0, M, 1)
+        gather_quoted(0, 0, M, 2)
+        quantise_w1(1, 0, [PASS])
+        round_w1(1, 1, 0)
+        gather_rebut(0, 0, M, 2)
+        gather_quoted(0, 0, M, 3)
+        quantise_w1(1, 1, [PASS])
+        for t in range(PACK):
+            first_stage_pass(1, t, 0)
+            first_stage_pass(1, t, 1)
+        gather_rebut(0, 0, M, 3)
+        round_x(0, 0, M)
+        for t in range(PACK):
+            fetch_h(1, t)
+        round_b(0, 0, M)
+        quantise_x(0, 0, M)
+
+        for number, (m0, mc) in enumerate(CHUNKS):
+            open_piece(1, m0, mc)
+            for t in range(PACK):
+                gather_quoted(1, m0, mc, t)
+            if number == 0:
+                quantise_b(0, 0, M)
+                for mt in range(M // P):
+                    second_stage_passes(0, 0, mt)
+            for t in range(PACK):
+                gather_rebut(1, m0, mc, t)
+            round_b(1, m0, mc)
+            round_x(1, m0, mc)
+            quantise_x(1, m0, mc)
+            quantise_b(1, m0, mc)
+            for mt in range(m0 // P, (m0 + mc) // P):
+                second_stage_passes(1, m0, mt)
+        for m0, mc in CHUNKS:
+            for half in range(2):
+                finish(m0, mc, half)

@@ -43,25 +43,21 @@ def tile_list_citation_chain_reader_kernel(
         pos1_sb = lists.tile([P, M // LIST_ROWS], U16)
         pos2_sb = lists.tile([P, M // LIST_ROWS], U16)
 
-        tab_sc = keep.tile([P, T], U8, align_bytes=64)
-        w2_sc = keep.tile([P, 2 * H], U8, align_bytes=64)
-        w3_sc = keep.tile([P, 2 * H], U8, align_bytes=64)
+        tab_sc = keep.tile([P, T], U8, tag="w1_bf00", align_bytes=64)
         nc.vector.memset(tab_sc[:].bitcast(I32), 0)
-        nc.vector.memset(w2_sc[:].bitcast(I32), 0)
-        nc.vector.memset(w3_sc[:].bitcast(I32), 0)
 
         warm = keep.tile([P, 8], F32)
         nc.vector.memset(warm[:], 0.0)
         nc.scalar.activation(warm[:], warm[:], ACT.Gelu_apprx_tanh)
 
-        tab_w = [keep.tile([P, T], I32, name="tab_w%d" % g, align_bytes=64) for g in range(2)]
+        tab_w = [keep.tile([P, T], I32, name="tab_w", tag="tab_w%d" % g, align_bytes=64) for g in range(2)]
         w1_raw = {}
 
         def load_table(g):
             nc.sync.dma_start(tab_w[g][:], tab_words[g].rearrange("p n i -> p (n i)").bitcast(I32))
 
-        def load_w1(a, g):
-            raw = keep.tile([P, PACK, PASS], F32, name="w1_raw%d%d" % (a, g))
+        def load_w1(a, g, tag):
+            raw = keep.tile([P, PACK, PASS], F32, name="w1_raw", tag=tag, align_bytes=64)
             rows = w1[g * PASS : (g + 1) * PASS, a * PASS : (a + 1) * PASS]
             nc.sync.dma_start(raw[:], rows.rearrange("(p j) c -> p j c", j=PACK))
             w1_raw[a, g] = raw
@@ -70,37 +66,44 @@ def tile_list_citation_chain_reader_kernel(
         gain_sb = keep.tile([P, 2, PACK], F32)
         skip_sb = keep.tile([P, 2, PACK], F32)
 
-        def load_factor(dst, vec):
-            nc.sync.dma_start(dst[:], vec.rearrange("(a p t) -> p a t", a=2, t=PACK))
-
         load_table(0)
         nc.sync.dma_start(offs_sb[:], offs)
-        load_w1(0, 0)
-        load_table(1)
-        load_w1(0, 1)
         nc.sync.dma_start(pos1_sb[:], pos1)
         nc.sync.dma_start(pos2_sb[:], pos2)
-        load_factor(tone_sb, tone)
-        load_w1(1, 0)
-        load_factor(gain_sb, gain)
-        load_w1(1, 1)
-        load_factor(skip_sb, skip)
-        w3_w = keep.tile([P, 2, H], I32, align_bytes=64)
-        nc.sync.dma_start(w3_w[:], w3_words.rearrange("a p n i -> p a (n i)").bitcast(I32))
-        w2_w = keep.tile([P, 2, 2 * H], U8, align_bytes=64)
-        nc.sync.dma_start(w2_w[:].bitcast(I32), w2_words.rearrange("a p n -> p a n").bitcast(I32))
-        for plane, rows in ((w3_sc, w3_scales), (w2_sc, w2_scales)):
-            for q in range(4):
-                nc.sync.dma_start(
-                    plane[32 * q : 32 * q + 4, :].bitcast(I32).rearrange("r (a n) -> r a n", a=2),
-                    rows[:, 4 * q : 4 * q + 4, :].rearrange("a r n -> r a n").bitcast(I32),
-                )
-
+        for dst, vec in ((tone_sb, tone), (gain_sb, gain), (skip_sb, skip)):
+            nc.sync.dma_start(dst[:], vec.rearrange("(a p t) -> p a t", a=2, t=PACK))
+        load_table(1)
+        load_w1(0, 0, "w1_raw0")
+        load_w1(0, 1, "w1_raw1")
         for q in range(4):
             nc.gpsimd.dma_start(
                 tab_sc[32 * q : 32 * q + 8, :].bitcast(I32),
                 tab_scales[:, 4 * q : 4 * q + 4, :].bitcast(I32),
             )
+
+        second = {}
+
+        def load_w3():
+            words = keep.tile([P, 2, H], I32, name="w3_w", tag="w1_raw0", align_bytes=64)
+            nc.sync.dma_start(words[:], w3_words.rearrange("a p n i -> p a (n i)").bitcast(I32))
+            second["w3"] = words
+
+        def load_w2():
+            words = keep.tile([P, 2, 2 * H], U8, name="w2_w", tag="w1_raw1", align_bytes=64)
+            nc.sync.dma_start(words[:].bitcast(I32), w2_words.rearrange("a p n -> p a n").bitcast(I32))
+            second["w2"] = words
+
+        def load_second_scales():
+            plane = keep.tile([P, 2 * H], U8, name="w23_sc", tag="w1_bf01", align_bytes=64)
+            nc.vector.memset(plane[:].bitcast(I32), 0)
+            for first, rows in ((4, w3_scales), (0, w2_scales)):
+                for q in range(4):
+                    nc.sync.dma_start(
+                        plane[32 * q + first : 32 * q + first + 4, :].bitcast(I32).rearrange("r (a n) -> r a n", a=2),
+                        rows[:, 4 * q : 4 * q + 4, :].rearrange("a r n -> r a n").bitcast(I32),
+                    )
+            second["scales"] = plane
+
         ident = keep.tile([P, P], F32)
         make_identity(nc, ident[:])
 
@@ -113,18 +116,19 @@ def tile_list_citation_chain_reader_kernel(
         w1_bf, w1_q = {}, {}
 
         def round_w1(a, g, vector_share):
-            grouped = keep.tile([P, PASS * PACK], BF16, name="w1_bf", tag="w1_bf", bufs=2, align_bytes=64)
+            grouped = keep.tile([P, PASS * PACK], BF16, name="w1_bf", tag="w1_bf%d%d" % (a, g), align_bytes=64)
             dst = grouped[:].rearrange("p (t m j) -> p m j t", t=PACK, j=PACK)
             src = w1_raw[a, g][:].rearrange("p j (m t) -> p m j t", t=PACK)
             if vector_share > 0:
                 nc.vector.tensor_copy(dst[:, :vector_share], src[:, :vector_share])
-            if vector_share < P:
                 nc.scalar.copy(dst[:, vector_share:], src[:, vector_share:])
+            else:
+                nc.gpsimd.tensor_scalar(dst, src, 1.0, 0.0, ALU.mult, ALU.add)
             w1_bf[a, g] = grouped
 
-        def quantise(name, values, widths):
+        def quantise(name, values, widths, tag=None):
             words = values.shape[1] // PACK
-            codes = keep.tile([P, words], U32, name=name + "_codes", align_bytes=64)
+            codes = keep.tile([P, words], U32, name=name + "_codes", tag=tag or name + "_codes", align_bytes=64)
             scales = keep.tile([P, words], U8, name=name + "_scales", align_bytes=64)
             c0 = 0
             for width in widths:
@@ -136,8 +140,8 @@ def tile_list_citation_chain_reader_kernel(
                 c0 += width
             return codes, scales
 
-        def quantise_w1(a, g, widths):
-            w1_q[a, g] = quantise("w1_%d%d" % (a, g), w1_bf[a, g], widths)
+        def quantise_w1(a, g, widths, tag=None):
+            w1_q[a, g] = quantise("w1_%d%d" % (a, g), w1_bf[a, g], widths, tag)
 
         h_acc, h = {}, {}
 
@@ -145,7 +149,7 @@ def tile_list_citation_chain_reader_kernel(
             codes, scales = w1_q[a, g]
             for half in range(2):
                 if g == 0:
-                    h_acc[a, t, half] = bank(2 * t + half, [P, BANK])
+                    h_acc[a, t, half] = bank(2 * (t % 2) + half, [P, BANK])
                 cols = slice(half * BANK, (half + 1) * BANK)
                 nc.tensor.matmul_mx(
                     out=h_acc[a, t, half][:],
@@ -158,7 +162,7 @@ def tile_list_citation_chain_reader_kernel(
                 )
 
         def fetch_h(a, t, vector_helps=False):
-            rows = keep.tile([P, S], F32, name="h%d%d" % (a, t))
+            rows = keep.tile([P, S], F32, name="h", tag="h%d%d" % (a, t), align_bytes=64)
             nc.scalar.copy(rows[:, :BANK], h_acc[a, t, 0][:])
             if vector_helps:
                 nc.vector.tensor_copy(rows[:, BANK:], h_acc[a, t, 1][:])
@@ -168,14 +172,19 @@ def tile_list_citation_chain_reader_kernel(
 
         quoted, rebut, x_q, b_q = {}, {}, {}, {}
 
-        def open_piece(a, m0, mc):
-            quoted[a, m0] = keep.tile([P, PACK, mc], F32, name="quoted%d_%d" % (a, m0))
-            rebut[a, m0] = keep.tile([P, PACK, mc], F32, name="rebut%d_%d" % (a, m0))
+        def open_quoted(a, m0, mc):
+            quoted[a, m0] = keep.tile([P, PACK, mc], F32, name="quoted", tag="quoted%d" % a)
+
+        def open_rebut(a, m0, mc, tag):
+            rebut[a, m0] = keep.tile([P, PACK, mc], F32, name="rebut", tag=tag, align_bytes=64)
 
         def gather_quoted(a, m0, mc, t):
             picks = pos1_sb[:, m0 // LIST_ROWS : (m0 + mc) // LIST_ROWS]
             d = quoted[a, m0][:, t, :]
             nc.vector.tensor_copy(d, h[a, t][:].indirect(picks))
+
+        def gelu(a, m0, t):
+            d = quoted[a, m0][:, t, :]
             nc.scalar.activation(d, d, ACT.Gelu_apprx_tanh, scale=tone_sb[:, a, t : t + 1])
 
         def gather_rebut(a, m0, mc, t):
@@ -191,14 +200,21 @@ def tile_list_citation_chain_reader_kernel(
             return tile[:].rearrange("p t (c i) -> p c t i", i=4)
 
         def round_x(a, m0, mc):
-            values = keep.tile([P, mc * PACK], BF16, name="x_bf%d_%d" % (a, m0), align_bytes=64)
+            values = keep.tile([P, mc * PACK], BF16, name="x_bf", tag="x_bf%d_%d" % (a, m0), align_bytes=64)
             factor = gain_sb[:, a, :].unsqueeze(1).unsqueeze(3).to_broadcast([P, mc // 4, PACK, 4])
             nc.vector.tensor_tensor(woven(values, mc), planes(quoted[a, m0]), factor, ALU.mult)
             x_bf[a, m0] = values
 
         def round_b(a, m0, mc):
-            values = keep.tile([P, mc * PACK], BF16, name="b_bf%d_%d" % (a, m0), align_bytes=64)
-            nc.scalar.copy(woven(values, mc), planes(rebut[a, m0]))
+            if a == 0:
+                values = keep.tile([P, mc * PACK], BF16, name="b_bf", tag="x_bf0_0", align_bytes=64)
+                nc.gpsimd.tensor_scalar(
+                    values[:].rearrange("p (m t) -> p m t", t=PACK), rebut[a, m0][:].rearrange("p t m -> p m t"),
+                    1.0, 0.0, ALU.mult, ALU.add,
+                )
+            else:
+                values = keep.tile([P, mc * PACK], BF16, name="b_bf%d_%d" % (a, m0), align_bytes=64)
+                nc.scalar.copy(woven(values, mc), planes(rebut[a, m0]))
             b_bf[a, m0] = values
 
         def quantise_x(a, m0, mc):
@@ -209,29 +225,34 @@ def tile_list_citation_chain_reader_kernel(
 
         y_acc = {}
 
-        def second_stage_passes(a, piece_m0, mt):
+        def x_passes(a, piece_m0, mt):
             c0 = mt * P - piece_m0
+            codes, scales = x_q[a, piece_m0]
             for half in range(2):
                 if a == 0:
-                    y_acc[mt, half] = bank(2 * mt + half, [P, BANK])
+                    y_acc[mt, half] = bank((2 * mt + half + 4) % 8, [P, BANK])
                 n0 = half * BANK
-                codes, scales = b_q[a, piece_m0]
                 nc.tensor.matmul_mx(
                     out=y_acc[mt, half][:],
                     lhsT=codes[:, c0 : c0 + P].bitcast(FP8X4),
                     lhsT_scale=scales[:, c0 : c0 + P],
-                    rhs=w3_w[:, a, n0 : n0 + BANK].bitcast(FP8X4),
-                    rhs_scale=w3_sc[:, a * H + n0 : a * H + n0 + BANK],
+                    rhs=second["w2"][:, a, 2 * n0 : 2 * (n0 + BANK)].bitcast(FP4X4),
+                    rhs_scale=second["scales"][:, a * H + n0 : a * H + n0 + BANK],
                     start=(a == 0),
                     stop=False,
                 )
-                codes, scales = x_q[a, piece_m0]
+
+        def b_passes(a, piece_m0, mt):
+            c0 = mt * P - piece_m0
+            codes, scales = b_q[a, piece_m0]
+            for half in range(2):
+                n0 = half * BANK
                 nc.tensor.matmul_mx(
                     out=y_acc[mt, half][:],
                     lhsT=codes[:, c0 : c0 + P].bitcast(FP8X4),
                     lhsT_scale=scales[:, c0 : c0 + P],
-                    rhs=w2_w[:, a, 2 * n0 : 2 * (n0 + BANK)].bitcast(FP4X4),
-                    rhs_scale=w2_sc[:, a * H + n0 : a * H + n0 + BANK],
+                    rhs=second["w3"][:, a, n0 : n0 + BANK].bitcast(FP8X4),
+                    rhs_scale=second["scales"][4:P, a * H + n0 : a * H + n0 + BANK],
                     start=False,
                     stop=(a == 1),
                 )
@@ -249,7 +270,7 @@ def tile_list_citation_chain_reader_kernel(
             piece_m0 = 0 if half == 0 else m0
             c0 = m0 - piece_m0
             for number, mt_bank in enumerate(tiles):
-                turned = bank(2 * mt_bank + half, [P, per_bank, mc])
+                turned = bank((2 * mt_bank + half + 4) % 8, [P, per_bank, mc])
                 for u in range(per_bank):
                     t = number * per_bank + u
                     for mt in tiles:
@@ -264,58 +285,68 @@ def tile_list_citation_chain_reader_kernel(
             nc.sync.dma_start(rows.rearrange("(p t) m -> p t m", t=PACK), result[:])
 
         gather_table(0)
+        load_w1(1, 0, "tab_w0")
         nc.vector.tensor_copy(v_sc[:], tab_sc[:].indirect(offs_sb[:]))
-        round_w1(0, 0, P)
+        gather_table(1)
+        load_w1(1, 1, "tab_w1")
+        round_w1(0, 0, VECTOR_SHARE)
+        load_w3()
         quantise_w1(0, 0, [PASS])
+        round_w1(0, 1, VECTOR_SHARE)
+        load_w2()
+        quantise_w1(0, 1, [P] * PACK)
+        load_second_scales()
         for t in range(PACK):
             first_stage_pass(0, t, 0)
-        gather_table(1)
-        round_w1(0, 1, VECTOR_SHARE)
-        quantise_w1(0, 1, [P] * PACK)
-        for t in range(PACK):
             first_stage_pass(0, t, 1)
-        open_piece(0, 0, M)
-        fetch_h(0, 0, vector_helps=True)
-        fetch_h(0, 1)
-        gather_quoted(0, 0, M, 0)
-        gather_rebut(0, 0, M, 0)
-        fetch_h(0, 2)
-        gather_quoted(0, 0, M, 1)
-        fetch_h(0, 3)
+        for t in range(PACK):
+            fetch_h(0, t, vector_helps=(t == 0))
         round_w1(1, 0, 0)
-        gather_rebut(0, 0, M, 1)
-        gather_quoted(0, 0, M, 2)
-        quantise_w1(1, 0, [PASS])
         round_w1(1, 1, 0)
-        gather_rebut(0, 0, M, 2)
-        gather_quoted(0, 0, M, 3)
-        quantise_w1(1, 1, [PASS])
+        open_quoted(0, 0, M)
+        open_rebut(0, 0, M, "rebut0")
+        for t in range(PACK):
+            gather_quoted(0, 0, M, t)
+            gather_rebut(0, 0, M, t)
+        quantise_w1(1, 0, [PASS], "h01")
+        quantise_w1(1, 1, [P] * PACK, "h02")
         for t in range(PACK):
             first_stage_pass(1, t, 0)
             first_stage_pass(1, t, 1)
-        gather_rebut(0, 0, M, 3)
+        for t in range(PACK):
+            gelu(0, 0, t)
         round_x(0, 0, M)
+        quantise_x(0, 0, M)
         for t in range(PACK):
             fetch_h(1, t)
+        for mt in range(M // P):
+            x_passes(0, 0, mt)
         round_b(0, 0, M)
-        quantise_x(0, 0, M)
 
         for number, (m0, mc) in enumerate(CHUNKS):
-            open_piece(1, m0, mc)
-            for t in range(PACK):
-                gather_quoted(1, m0, mc, t)
+            open_quoted(1, m0, mc)
+            open_rebut(1, m0, mc, "rebut1" if number == 0 else "x_bf1_0")
             if number == 0:
+                for t in range(PACK):
+                    gather_quoted(1, m0, mc, t)
+                    gather_rebut(1, m0, mc, t)
                 quantise_b(0, 0, M)
                 for mt in range(M // P):
-                    second_stage_passes(0, 0, mt)
+                    b_passes(0, 0, mt)
+            else:
+                for t in range(PACK):
+                    gather_quoted(1, m0, mc, t)
+                for t in range(PACK):
+                    gather_rebut(1, m0, mc, t)
             for t in range(PACK):
-                gather_rebut(1, m0, mc, t)
-            round_b(1, m0, mc)
+                gelu(1, m0, t)
             round_x(1, m0, mc)
+            round_b(1, m0, mc)
             quantise_x(1, m0, mc)
             quantise_b(1, m0, mc)
             for mt in range(m0 // P, (m0 + mc) // P):
-                second_stage_passes(1, m0, mt)
+                x_passes(1, m0, mt)
+                b_passes(1, m0, mt)
         for m0, mc in CHUNKS:
             for half in range(2):
                 finish(m0, mc, half)

@@ -23,7 +23,8 @@ PASS = P * PACK
 BANK = 512
 LIST_ROWS = 16
 CHUNKS = ((0, 256), (256, 256))
-VECTOR_SHARE = 88
+VECTOR_SHARE = 44
+CLEAR_SPLIT = 512
 
 
 def tile_list_citation_chain_reader_kernel(
@@ -43,66 +44,73 @@ def tile_list_citation_chain_reader_kernel(
         pos1_sb = lists.tile([P, M // LIST_ROWS], U16)
         pos2_sb = lists.tile([P, M // LIST_ROWS], U16)
 
-        tab_sc = keep.tile([P, T], U8, tag="w1_bf00", align_bytes=64)
-        nc.vector.memset(tab_sc[:].bitcast(I32), 0)
+        tab_sc = keep.tile([P, T], U8, tag="tab_sc", align_bytes=64)
+        nc.gpsimd.memset(tab_sc[:].bitcast(I32)[:, :CLEAR_SPLIT], 0)
+        nc.vector.memset(tab_sc[:].bitcast(I32)[:, CLEAR_SPLIT:], 0)
 
         warm = keep.tile([P, 8], F32)
         nc.vector.memset(warm[:], 0.0)
         nc.scalar.activation(warm[:], warm[:], ACT.Gelu_apprx_tanh)
 
-        tab_w = [keep.tile([P, T], I32, name="tab_w", tag="tab_w%d" % g, align_bytes=64) for g in range(2)]
-        w1_raw = {}
+        tab_w = [keep.tile([P, T], I32, name="tab_w%d" % g, align_bytes=64) for g in range(2)]
+        w1_raw, w1_part = {}, {}
 
-        def load_table(g):
-            nc.sync.dma_start(tab_w[g][:], tab_words[g].rearrange("p n i -> p (n i)").bitcast(I32))
+        def load_table(g, c0, c1):
+            words = tab_words[g].rearrange("p n i -> p (n i)").bitcast(I32)
+            nc.sync.dma_start(tab_w[g][:, c0:c1], words[:, c0:c1])
 
-        def load_w1(a, g, tag):
-            raw = keep.tile([P, PACK, PASS], F32, name="w1_raw", tag=tag, align_bytes=64)
-            rows = w1[g * PASS : (g + 1) * PASS, a * PASS : (a + 1) * PASS]
-            nc.sync.dma_start(raw[:], rows.rearrange("(p j) c -> p j c", j=PACK))
-            w1_raw[a, g] = raw
+        def load_w1(a, g, parts):
+            if g == 0:
+                w1_raw[a] = keep.tile([P, 2 * PACK * PASS], F32, name="w1_raw", tag="w1_raw%d" % a)
+            width = PASS // parts
+            for c0 in range(0, PASS, width):
+                first = (g * PASS + c0) * PACK
+                part = w1_raw[a][:, first : first + PACK * width].rearrange("p (j c) -> p j c", j=PACK)
+                rows = w1[g * PASS : (g + 1) * PASS, a * PASS + c0 : a * PASS + c0 + width]
+                nc.sync.dma_start(part, rows.rearrange("(p j) c -> p j c", j=PACK))
+                w1_part[a, g, c0] = part
 
         tone_sb = keep.tile([P, 2, PACK], F32)
         gain_sb = keep.tile([P, 2, PACK], F32)
         skip_sb = keep.tile([P, 2, PACK], F32)
 
-        load_table(0)
+        def load_table_scales(g):
+            for q in range(4):
+                nc.sync.dma_start(
+                    tab_sc[32 * q + 4 * g : 32 * q + 4 * g + 4, :].bitcast(I32),
+                    tab_scales[g, 4 * q : 4 * q + 4, :].bitcast(I32),
+                )
+
+        def load_factor(dst, vec):
+            nc.sync.dma_start(dst[:], vec.rearrange("(a p t) -> p a t", a=2, t=PACK))
+
+        load_table(0, 0, T // 2)
         nc.sync.dma_start(offs_sb[:], offs)
+        load_table(0, T // 2, T)
+        load_table_scales(0)
+        load_w1(0, 0, 1)
+        load_table_scales(1)
+        load_table(1, 0, T)
+        load_w1(0, 1, 2)
         nc.sync.dma_start(pos1_sb[:], pos1)
         nc.sync.dma_start(pos2_sb[:], pos2)
-        for dst, vec in ((tone_sb, tone), (gain_sb, gain), (skip_sb, skip)):
-            nc.sync.dma_start(dst[:], vec.rearrange("(a p t) -> p a t", a=2, t=PACK))
-        load_table(1)
-        load_w1(0, 0, "w1_raw0")
-        load_w1(0, 1, "w1_raw1")
-        for q in range(4):
-            nc.gpsimd.dma_start(
-                tab_sc[32 * q : 32 * q + 8, :].bitcast(I32),
-                tab_scales[:, 4 * q : 4 * q + 4, :].bitcast(I32),
-            )
-
-        second = {}
-
-        def load_w3():
-            words = keep.tile([P, 2, H], I32, name="w3_w", tag="w1_raw0", align_bytes=64)
-            nc.sync.dma_start(words[:], w3_words.rearrange("a p n i -> p a (n i)").bitcast(I32))
-            second["w3"] = words
-
-        def load_w2():
-            words = keep.tile([P, 2, 2 * H], U8, name="w2_w", tag="w1_raw1", align_bytes=64)
-            nc.sync.dma_start(words[:].bitcast(I32), w2_words.rearrange("a p n -> p a n").bitcast(I32))
-            second["w2"] = words
-
-        def load_second_scales():
-            plane = keep.tile([P, 2 * H], U8, name="w23_sc", tag="w1_bf01", align_bytes=64)
-            nc.vector.memset(plane[:].bitcast(I32), 0)
-            for first, rows in ((4, w3_scales), (0, w2_scales)):
-                for q in range(4):
-                    nc.sync.dma_start(
-                        plane[32 * q + first : 32 * q + first + 4, :].bitcast(I32).rearrange("r (a n) -> r a n", a=2),
-                        rows[:, 4 * q : 4 * q + 4, :].rearrange("a r n -> r a n").bitcast(I32),
-                    )
-            second["scales"] = plane
+        load_factor(tone_sb, tone)
+        load_w1(1, 0, 1)
+        load_w1(1, 1, 1)
+        load_factor(gain_sb, gain)
+        load_factor(skip_sb, skip)
+        w2_w = keep.tile([P, 2, 2 * H], U8, align_bytes=64)
+        nc.sync.dma_start(w2_w[:].bitcast(I32), w2_words.rearrange("a p n -> p a n").bitcast(I32))
+        w3_w = keep.tile([P, 2, H], I32, align_bytes=64)
+        nc.sync.dma_start(w3_w[:], w3_words.rearrange("a p n i -> p a (n i)").bitcast(I32))
+        w23_sc = keep.tile([P, 2 * H], U8, align_bytes=64)
+        nc.vector.memset(w23_sc[:].bitcast(I32), 0)
+        for first, rows in ((0, w2_scales), (4, w3_scales)):
+            for q in range(4):
+                nc.sync.dma_start(
+                    w23_sc[32 * q + first : 32 * q + first + 4, :].bitcast(I32).rearrange("r (a n) -> r a n", a=2),
+                    rows[:, 4 * q : 4 * q + 4, :].rearrange("a r n -> r a n").bitcast(I32),
+                )
 
         ident = keep.tile([P, P], F32)
         make_identity(nc, ident[:])
@@ -114,17 +122,19 @@ def tile_list_citation_chain_reader_kernel(
             nc.vector.tensor_copy(v_w[g][:], tab_w[g][:].bitcast(U32).indirect(offs_sb[:]))
 
         w1_bf, w1_q = {}, {}
+        first_picks = [keep.tile([P, (PACK + 1) * M], F32, name="picks%d" % g, align_bytes=64) for g in range(2)]
+        for g in range(2):
+            w1_bf[1, g] = first_picks[g][:, (PACK - 1) * M :].bitcast(BF16)
 
-        def round_w1(a, g, vector_share):
-            grouped = keep.tile([P, PASS * PACK], BF16, name="w1_bf", tag="w1_bf%d%d" % (a, g), align_bytes=64)
-            dst = grouped[:].rearrange("p (t m j) -> p m j t", t=PACK, j=PACK)
-            src = w1_raw[a, g][:].rearrange("p j (m t) -> p m j t", t=PACK)
+        def round_w1(a, g, c0, vector_share):
+            if c0 == 0 and a == 0:
+                w1_bf[a, g] = keep.tile([P, PASS * PACK], BF16, name="w1_bf%d%d" % (a, g), align_bytes=64)
+            src = w1_part[a, g, c0].rearrange("p j (m t) -> p m j t", t=PACK)
+            dst = w1_bf[a, g][:].rearrange("p (t m j) -> p m j t", t=PACK, j=PACK)
+            dst = dst[:, c0 // PACK : c0 // PACK + src.shape[1]]
             if vector_share > 0:
                 nc.vector.tensor_copy(dst[:, :vector_share], src[:, :vector_share])
-                nc.scalar.copy(dst[:, vector_share:], src[:, vector_share:])
-            else:
-                nc.gpsimd.tensor_scalar(dst, src, 1.0, 0.0, ALU.mult, ALU.add)
-            w1_bf[a, g] = grouped
+            nc.scalar.copy(dst[:, vector_share:], src[:, vector_share:])
 
         def quantise(name, values, widths, tag=None):
             words = values.shape[1] // PACK
@@ -149,7 +159,7 @@ def tile_list_citation_chain_reader_kernel(
             codes, scales = w1_q[a, g]
             for half in range(2):
                 if g == 0:
-                    h_acc[a, t, half] = bank(2 * (t % 2) + half, [P, BANK])
+                    h_acc[a, t, half] = bank(2 * (t % 2) + half + (4 if a == 1 and t < 2 else 0), [P, BANK])
                 cols = slice(half * BANK, (half + 1) * BANK)
                 nc.tensor.matmul_mx(
                     out=h_acc[a, t, half][:],
@@ -170,7 +180,7 @@ def tile_list_citation_chain_reader_kernel(
                 nc.scalar.copy(rows[:, BANK:], h_acc[a, t, 1][:])
             h[a, t] = rows
 
-        quoted, rebut, x_q, b_q = {}, {}, {}, {}
+        quoted, curved, rebut, x_q, b_q = {}, {}, {}, {}, {}
 
         def open_quoted(a, m0, mc):
             quoted[a, m0] = keep.tile([P, PACK, mc], F32, name="quoted", tag="quoted%d" % a)
@@ -185,7 +195,11 @@ def tile_list_citation_chain_reader_kernel(
 
         def gelu(a, m0, t):
             d = quoted[a, m0][:, t, :]
-            nc.scalar.activation(d, d, ACT.Gelu_apprx_tanh, scale=tone_sb[:, a, t : t + 1])
+            if a == 0 and t == 0:
+                curved[a, m0] = keep.tile([P, PACK, M], F32, name="curved", tag="w1_raw1")
+            if a == 1:
+                curved[a, m0] = quoted[a, m0]
+            nc.scalar.activation(curved[a, m0][:, t, :], d, ACT.Gelu_apprx_tanh, scale=tone_sb[:, a, t : t + 1])
 
         def gather_rebut(a, m0, mc, t):
             picks = pos2_sb[:, m0 // LIST_ROWS : (m0 + mc) // LIST_ROWS]
@@ -202,19 +216,12 @@ def tile_list_citation_chain_reader_kernel(
         def round_x(a, m0, mc):
             values = keep.tile([P, mc * PACK], BF16, name="x_bf", tag="x_bf%d_%d" % (a, m0), align_bytes=64)
             factor = gain_sb[:, a, :].unsqueeze(1).unsqueeze(3).to_broadcast([P, mc // 4, PACK, 4])
-            nc.vector.tensor_tensor(woven(values, mc), planes(quoted[a, m0]), factor, ALU.mult)
+            nc.vector.tensor_tensor(woven(values, mc), planes(curved[a, m0]), factor, ALU.mult)
             x_bf[a, m0] = values
 
-        def round_b(a, m0, mc):
-            if a == 0:
-                values = keep.tile([P, mc * PACK], BF16, name="b_bf", tag="x_bf0_0", align_bytes=64)
-                nc.gpsimd.tensor_scalar(
-                    values[:].rearrange("p (m t) -> p m t", t=PACK), rebut[a, m0][:].rearrange("p t m -> p m t"),
-                    1.0, 0.0, ALU.mult, ALU.add,
-                )
-            else:
-                values = keep.tile([P, mc * PACK], BF16, name="b_bf%d_%d" % (a, m0), align_bytes=64)
-                nc.scalar.copy(woven(values, mc), planes(rebut[a, m0]))
+        def round_b(a, m0, mc, tag):
+            values = keep.tile([P, mc * PACK], BF16, name="b_bf", tag=tag, align_bytes=64)
+            nc.scalar.copy(woven(values, mc), planes(rebut[a, m0]))
             b_bf[a, m0] = values
 
         def quantise_x(a, m0, mc):
@@ -225,91 +232,93 @@ def tile_list_citation_chain_reader_kernel(
 
         y_acc = {}
 
-        def x_passes(a, piece_m0, mt):
+        def x_pass(a, piece_m0, mt, half):
             c0 = mt * P - piece_m0
             codes, scales = x_q[a, piece_m0]
-            for half in range(2):
-                if a == 0:
-                    y_acc[mt, half] = bank((2 * mt + half + 4) % 8, [P, BANK])
-                n0 = half * BANK
-                nc.tensor.matmul_mx(
-                    out=y_acc[mt, half][:],
-                    lhsT=codes[:, c0 : c0 + P].bitcast(FP8X4),
-                    lhsT_scale=scales[:, c0 : c0 + P],
-                    rhs=second["w2"][:, a, 2 * n0 : 2 * (n0 + BANK)].bitcast(FP4X4),
-                    rhs_scale=second["scales"][:, a * H + n0 : a * H + n0 + BANK],
-                    start=(a == 0),
-                    stop=False,
-                )
+            if a == 0:
+                y_acc[mt, half] = bank((2 * mt + half + 4) % 8, [P, BANK])
+            n0 = half * BANK
+            nc.tensor.matmul_mx(
+                out=y_acc[mt, half][:],
+                lhsT=codes[:, c0 : c0 + P].bitcast(FP8X4),
+                lhsT_scale=scales[:, c0 : c0 + P],
+                rhs=w2_w[:, a, 2 * n0 : 2 * (n0 + BANK)].bitcast(FP4X4),
+                rhs_scale=w23_sc[:, a * H + n0 : a * H + n0 + BANK],
+                start=(a == 0),
+                stop=False,
+            )
 
-        def b_passes(a, piece_m0, mt):
+        def b_pass(a, piece_m0, mt, half):
             c0 = mt * P - piece_m0
             codes, scales = b_q[a, piece_m0]
-            for half in range(2):
-                n0 = half * BANK
-                nc.tensor.matmul_mx(
-                    out=y_acc[mt, half][:],
-                    lhsT=codes[:, c0 : c0 + P].bitcast(FP8X4),
-                    lhsT_scale=scales[:, c0 : c0 + P],
-                    rhs=second["w3"][:, a, n0 : n0 + BANK].bitcast(FP8X4),
-                    rhs_scale=second["scales"][4:P, a * H + n0 : a * H + n0 + BANK],
-                    start=False,
-                    stop=(a == 1),
-                )
+            n0 = half * BANK
+            nc.tensor.matmul_mx(
+                out=y_acc[mt, half][:],
+                lhsT=codes[:, c0 : c0 + P].bitcast(FP8X4),
+                lhsT_scale=scales[:, c0 : c0 + P],
+                rhs=w3_w[:, a, n0 : n0 + BANK].bitcast(FP8X4),
+                rhs_scale=w23_sc[4:P, a * H + n0 : a * H + n0 + BANK],
+                start=False,
+                stop=(a == 1),
+            )
 
-        def finish(m0, mc, half):
+        turned = {}
+
+        def turn(m0, mc, half):
             tiles = range(m0 // P, (m0 + mc) // P)
             bent = {}
             for mt in tiles:
-                bent[mt] = keep.tile([P, PACK, P], F32, name="bent", tag="bent", bufs=4)
+                bent[mt] = keep.tile([P, PACK, P], F32, name="bent", tag="bent%d%d" % (mt, half), align_bytes=64)
                 nc.scalar.activation(
                     bent[mt][:], y_acc[mt, half][:].rearrange("m (p t) -> m t p", t=PACK), ACT.Tanh
                 )
             per_bank = PACK // len(tiles)
-            result = keep.tile([P, PACK, mc], F32, name="result%d_%d" % (half, m0))
-            piece_m0 = 0 if half == 0 else m0
-            c0 = m0 - piece_m0
             for number, mt_bank in enumerate(tiles):
-                turned = bank((2 * mt_bank + half + 4) % 8, [P, per_bank, mc])
+                target = bank((2 * mt_bank + half + 4) % 8, [P, per_bank, mc])
                 for u in range(per_bank):
                     t = number * per_bank + u
                     for mt in tiles:
-                        nc.tensor.transpose(turned[:, u, mt * P - m0 : (mt + 1) * P - m0], bent[mt][:, t, :], ident[:])
-                for u in range(per_bank):
-                    t = number * per_bank + u
-                    nc.vector.scalar_tensor_tensor(
-                        result[:, t, :], rebut[half, piece_m0][:, t, c0 : c0 + mc], skip_sb[:, half, t : t + 1],
-                        turned[:, u, :], ALU.mult, ALU.add,
-                    )
-            rows = out[half * PASS : (half + 1) * PASS, m0 : m0 + mc]
-            nc.sync.dma_start(rows.rearrange("(p t) m -> p t m", t=PACK), result[:])
+                        nc.tensor.transpose(target[:, u, mt * P - m0 : (mt + 1) * P - m0], bent[mt][:, t, :], ident[:])
+                    turned[m0, half, t] = target[:, u, :]
+
+        def finish(m0, mc, half, tag, per_store):
+            result = keep.tile([P, PACK, mc], F32, name="result", tag=tag, align_bytes=64)
+            piece_m0 = 0 if half == 0 else m0
+            c0 = m0 - piece_m0
+            rows = out[half * PASS : (half + 1) * PASS, m0 : m0 + mc].rearrange("(p t) m -> p t m", t=PACK)
+            for t in range(PACK):
+                nc.vector.scalar_tensor_tensor(
+                    result[:, t, :], rebut[half, piece_m0][:, t, c0 : c0 + mc], skip_sb[:, half, t : t + 1],
+                    turned[m0, half, t], ALU.mult, ALU.add,
+                )
+                if (t + 1) % per_store == 0:
+                    done = slice(t + 1 - per_store, t + 1)
+                    nc.sync.dma_start(rows[:, done, :], result[:, done, :])
 
         gather_table(0)
-        load_w1(1, 0, "tab_w0")
         nc.vector.tensor_copy(v_sc[:], tab_sc[:].indirect(offs_sb[:]))
+        round_w1(0, 0, 0, 0)
+        quantise_w1(0, 0, [PASS], "tab_sc")
         gather_table(1)
-        load_w1(1, 1, "tab_w1")
-        round_w1(0, 0, VECTOR_SHARE)
-        load_w3()
-        quantise_w1(0, 0, [PASS])
-        round_w1(0, 1, VECTOR_SHARE)
-        load_w2()
+        round_w1(0, 1, 0, 0)
+        round_w1(0, 1, PASS // 2, VECTOR_SHARE)
         quantise_w1(0, 1, [P] * PACK)
-        load_second_scales()
         for t in range(PACK):
             first_stage_pass(0, t, 0)
             first_stage_pass(0, t, 1)
         for t in range(PACK):
             fetch_h(0, t, vector_helps=(t == 0))
-        round_w1(1, 0, 0)
-        round_w1(1, 1, 0)
-        open_quoted(0, 0, M)
-        open_rebut(0, 0, M, "rebut0")
-        for t in range(PACK):
+        round_w1(1, 0, 0, 0)
+        round_w1(1, 1, 0, 0)
+        quoted[0, 0] = first_picks[0][:, : PACK * M].rearrange("p (t m) -> p t m", t=PACK)
+        rebut[0, 0] = first_picks[1][:, : PACK * M].rearrange("p (t m) -> p t m", t=PACK)
+        for t in range(PACK - 1):
             gather_quoted(0, 0, M, t)
             gather_rebut(0, 0, M, t)
-        quantise_w1(1, 0, [PASS], "h01")
-        quantise_w1(1, 1, [P] * PACK, "h02")
+        quantise_w1(1, 0, [PASS])
+        gather_quoted(0, 0, M, PACK - 1)
+        quantise_w1(1, 1, [PASS])
+        gather_rebut(0, 0, M, PACK - 1)
         for t in range(PACK):
             first_stage_pass(1, t, 0)
             first_stage_pass(1, t, 1)
@@ -320,33 +329,52 @@ def tile_list_citation_chain_reader_kernel(
         for t in range(PACK):
             fetch_h(1, t)
         for mt in range(M // P):
-            x_passes(0, 0, mt)
-        round_b(0, 0, M)
-
-        for number, (m0, mc) in enumerate(CHUNKS):
-            open_quoted(1, m0, mc)
-            open_rebut(1, m0, mc, "rebut1" if number == 0 else "x_bf1_0")
-            if number == 0:
-                for t in range(PACK):
-                    gather_quoted(1, m0, mc, t)
-                    gather_rebut(1, m0, mc, t)
-                quantise_b(0, 0, M)
-                for mt in range(M // P):
-                    b_passes(0, 0, mt)
-            else:
-                for t in range(PACK):
-                    gather_quoted(1, m0, mc, t)
-                for t in range(PACK):
-                    gather_rebut(1, m0, mc, t)
-            for t in range(PACK):
-                gelu(1, m0, t)
-            round_x(1, m0, mc)
-            round_b(1, m0, mc)
-            quantise_x(1, m0, mc)
-            quantise_b(1, m0, mc)
-            for mt in range(m0 // P, (m0 + mc) // P):
-                x_passes(1, m0, mt)
-                b_passes(1, m0, mt)
-        for m0, mc in CHUNKS:
             for half in range(2):
-                finish(m0, mc, half)
+                x_pass(0, 0, mt, half)
+        round_b(0, 0, M, "b_bf0")
+
+        def last_passes(m0, mc):
+            for half in range(2):
+                for mt in range(m0 // P, (m0 + mc) // P):
+                    x_pass(1, m0, mt, half)
+                for mt in range(m0 // P, (m0 + mc) // P):
+                    b_pass(1, m0, mt, half)
+
+        (m0, mc), (m1, md) = CHUNKS
+        open_quoted(1, m0, mc)
+        open_rebut(1, m0, mc, "rebut1")
+        for t in range(PACK):
+            gather_quoted(1, m0, mc, t)
+            gather_rebut(1, m0, mc, t)
+        quantise_b(0, 0, M)
+        for mt in range(M // P):
+            for half in range(2):
+                b_pass(0, 0, mt, half)
+        for t in range(PACK):
+            gelu(1, m0, t)
+        round_x(1, m0, mc)
+        round_b(1, m0, mc, "b_bf1")
+        quantise_x(1, m0, mc)
+        quantise_b(1, m0, mc)
+        last_passes(m0, mc)
+
+        open_quoted(1, m1, md)
+        open_rebut(1, m1, md, "x_bf1_0")
+        for t in range(PACK):
+            gather_quoted(1, m1, md, t)
+        for t in range(PACK):
+            gather_rebut(1, m1, md, t)
+        for t in range(PACK):
+            gelu(1, m1, t)
+        for half in range(2):
+            turn(m0, mc, half)
+        round_x(1, m1, md)
+        round_b(1, m1, md, "bent11")
+        quantise_x(1, m1, md)
+        quantise_b(1, m1, md)
+        last_passes(m1, md)
+        finish(m0, mc, 0, "bent11", PACK)
+        finish(m0, mc, 1, "x_bf1_256", PACK)
+        for half in range(2):
+            turn(m1, md, half)
+            finish(m1, md, half, "result%d" % half, 2)

@@ -23,7 +23,7 @@ PASS = P * PACK
 BANK = 512
 LIST_ROWS = 16
 CHUNKS = ((0, 256), (256, 256))
-VECTOR_SHARE = 44
+VECTOR_SHARE = 40
 CLEAR_SPLIT = 512
 
 
@@ -70,26 +70,26 @@ def tile_list_citation_chain_reader_kernel(
                 nc.sync.dma_start(part, rows.rearrange("(p j) c -> p j c", j=PACK))
                 w1_part[a, g, c0] = part
 
-        tone_sb = keep.tile([P, 2, PACK], F32)
-        gain_sb = keep.tile([P, 2, PACK], F32)
-        skip_sb = keep.tile([P, 2, PACK], F32)
+        tone_sb = keep.tile([P, 2, 2 * PACK], F32)
+        gain_sb = keep.tile([P, 2, 2 * PACK], F32)
+        skip_sb = keep.tile([P, 2, 2 * PACK], F32)
 
-        def load_table_scales(g):
-            for q in range(4):
-                nc.sync.dma_start(
-                    tab_sc[32 * q + 4 * g : 32 * q + 4 * g + 4, :].bitcast(I32),
-                    tab_scales[g, 4 * q : 4 * q + 4, :].bitcast(I32),
-                )
+        def load_table_scales(rows):
+            for r in rows:
+                for g in range(2):
+                    nc.sync.dma_start(
+                        tab_sc[4 * g + r : P : 32, :].bitcast(I32), tab_scales[g, r:16:4, :].bitcast(I32)
+                    )
 
         def load_factor(dst, vec):
-            nc.sync.dma_start(dst[:], vec.rearrange("(a p t) -> p a t", a=2, t=PACK))
+            nc.sync.dma_start(dst[:, :, :PACK], vec.rearrange("(a p t) -> p a t", a=2, t=PACK))
 
         load_table(0, 0, T // 2)
         nc.sync.dma_start(offs_sb[:], offs)
         load_table(0, T // 2, T)
-        load_table_scales(0)
+        load_table_scales((0, 1))
         load_w1(0, 0, 1)
-        load_table_scales(1)
+        load_table_scales((2, 3))
         load_table(1, 0, T)
         load_w1(0, 1, 2)
         nc.sync.dma_start(pos1_sb[:], pos1)
@@ -105,11 +105,11 @@ def tile_list_citation_chain_reader_kernel(
         nc.sync.dma_start(w3_w[:], w3_words.rearrange("a p n i -> p a (n i)").bitcast(I32))
         w23_sc = keep.tile([P, 2 * H], U8, align_bytes=64)
         nc.vector.memset(w23_sc[:].bitcast(I32), 0)
-        for first, rows in ((0, w2_scales), (4, w3_scales)):
-            for q in range(4):
+        for r in range(4):
+            for first, rows in ((0, w2_scales), (4, w3_scales)):
                 nc.sync.dma_start(
-                    w23_sc[32 * q + first : 32 * q + first + 4, :].bitcast(I32).rearrange("r (a n) -> r a n", a=2),
-                    rows[:, 4 * q : 4 * q + 4, :].rearrange("a r n -> r a n").bitcast(I32),
+                    w23_sc[first + r : P : 32, :].bitcast(I32).rearrange("q (a n) -> q a n", a=2),
+                    rows[:, r:16:4, :].rearrange("a q n -> q a n").bitcast(I32),
                 )
 
         ident = keep.tile([P, P], F32)
@@ -215,8 +215,9 @@ def tile_list_citation_chain_reader_kernel(
 
         def round_x(a, m0, mc):
             values = keep.tile([P, mc * PACK], BF16, name="x_bf", tag="x_bf%d_%d" % (a, m0), align_bytes=64)
-            factor = gain_sb[:, a, :].unsqueeze(1).unsqueeze(3).to_broadcast([P, mc // 4, PACK, 4])
-            nc.vector.tensor_tensor(woven(values, mc), planes(curved[a, m0]), factor, ALU.mult)
+            factor = gain_sb[:, a, :PACK].unsqueeze(1).unsqueeze(3).to_broadcast([P, mc // 8, PACK, 4])
+            for part in (slice(0, mc // 8), slice(mc // 8, mc // 4)):
+                nc.vector.tensor_tensor(woven(values, mc)[:, part], planes(curved[a, m0])[:, part], factor, ALU.mult)
             x_bf[a, m0] = values
 
         def round_b(a, m0, mc, tag):
@@ -225,7 +226,7 @@ def tile_list_citation_chain_reader_kernel(
             b_bf[a, m0] = values
 
         def quantise_x(a, m0, mc):
-            x_q[a, m0] = quantise("x%d_%d" % (a, m0), x_bf[a, m0], [mc])
+            x_q[a, m0] = quantise("x%d_%d" % (a, m0), x_bf[a, m0], [mc // 2, mc // 2])
 
         def quantise_b(a, m0, mc):
             b_q[a, m0] = quantise("b%d_%d" % (a, m0), b_bf[a, m0], [mc])
@@ -270,7 +271,9 @@ def tile_list_citation_chain_reader_kernel(
             for mt in tiles:
                 bent[mt] = keep.tile([P, PACK, P], F32, name="bent", tag="bent%d%d" % (mt, half), align_bytes=64)
                 nc.scalar.activation(
-                    bent[mt][:], y_acc[mt, half][:].rearrange("m (p t) -> m t p", t=PACK), ACT.Tanh
+                    bent[mt][:].rearrange("m t p -> m p t"),
+                    y_acc[mt, half][:].rearrange("m (p t) -> m p t", t=PACK),
+                    ACT.Tanh,
                 )
             per_bank = PACK // len(tiles)
             for number, mt_bank in enumerate(tiles):

@@ -134,7 +134,15 @@ def tile_list_citation_chain_reader_kernel(
             dst = dst[:, c0 // PACK : c0 // PACK + src.shape[1]]
             if vector_share > 0:
                 nc.vector.tensor_copy(dst[:, :vector_share], src[:, :vector_share])
-            nc.scalar.copy(dst[:, vector_share:], src[:, vector_share:])
+            if a == 1:
+                half = src.shape[1] // 2
+                for part in (slice(0, half), slice(half, 2 * half)):
+                    nc.gpsimd.tensor_scalar(
+                        dst[:, part].rearrange("p m j t -> p t m j"), src[:, part].rearrange("p m j t -> p t m j"),
+                        1.0, 0.0, ALU.mult, ALU.add,
+                    )
+            else:
+                nc.scalar.copy(dst[:, vector_share:], src[:, vector_share:])
 
         def quantise(name, values, widths, tag=None):
             words = values.shape[1] // PACK

@@ -1,7 +1,6 @@
 from contextlib import ExitStack
 
 import concourse.mybir as mybir
-from concourse.masks import make_identity
 
 K, H, T, S, M = 1024, 1024, 4096, 1024, 512
 FLOPS = 2 * K * H * S + 2 * 2 * H * H * M
@@ -52,7 +51,7 @@ def tile_list_citation_chain_reader_kernel(
         nc.vector.memset(warm[:], 0.0)
         nc.scalar.activation(warm[:], warm[:], ACT.Gelu_apprx_tanh)
 
-        tab_w = [keep.tile([P, T], I32, name="tab_w%d" % g, align_bytes=64) for g in range(2)]
+        tab_w = [keep.tile([P, T], I32, name="tab_w", tag="tab_w%d" % g, align_bytes=64) for g in range(2)]
         w1_raw, w1_part = {}, {}
 
         def load_table(g, c0, c1):
@@ -61,10 +60,10 @@ def tile_list_citation_chain_reader_kernel(
 
         def load_w1(a, g, parts):
             if g == 0:
-                w1_raw[a] = keep.tile([P, 2 * PACK * PASS], F32, name="w1_raw", tag="w1_raw%d" % a)
+                w1_raw[a] = keep.tile([P, 3 * PACK * PASS], F32, name="w1_raw", tag="w1_raw%d" % a, align_bytes=64)
             width = PASS // parts
             for c0 in range(0, PASS, width):
-                first = (g * PASS + c0) * PACK
+                first = (2 * g * PASS + c0) * PACK
                 part = w1_raw[a][:, first : first + PACK * width].rearrange("p (j c) -> p j c", j=PACK)
                 rows = w1[g * PASS : (g + 1) * PASS, a * PASS + c0 : a * PASS + c0 + width]
                 nc.sync.dma_start(part, rows.rearrange("(p j) c -> p j c", j=PACK))
@@ -72,7 +71,7 @@ def tile_list_citation_chain_reader_kernel(
 
         tone_sb = keep.tile([P, 2, 2 * PACK], F32)
         gain_sb = keep.tile([P, 2, 2 * PACK], F32)
-        skip_sb = keep.tile([P, 2, 2 * PACK], F32)
+        skip_sb = keep.tile([P, H // P], F32)
 
         def load_table_scales(rows):
             for r in rows:
@@ -94,11 +93,10 @@ def tile_list_citation_chain_reader_kernel(
         load_w1(0, 1, 2)
         nc.sync.dma_start(pos1_sb[:], pos1)
         nc.sync.dma_start(pos2_sb[:], pos2)
-        load_factor(tone_sb, tone)
         load_w1(1, 0, 1)
         load_w1(1, 1, 1)
+        load_factor(tone_sb, tone)
         load_factor(gain_sb, gain)
-        load_factor(skip_sb, skip)
         w2_w = keep.tile([P, 2, 2 * H], U8, align_bytes=64)
         nc.sync.dma_start(w2_w[:].bitcast(I32), w2_words.rearrange("a p n -> p a n").bitcast(I32))
         w3_w = keep.tile([P, 2, H], I32, align_bytes=64)
@@ -112,8 +110,8 @@ def tile_list_citation_chain_reader_kernel(
                     rows[:, r:16:4, :].rearrange("a q n -> q a n").bitcast(I32),
                 )
 
-        ident = keep.tile([P, P], F32)
-        make_identity(nc, ident[:])
+        with nc.allow_non_contiguous_dma(reason="one factor for each partition and row tile"):
+            nc.sync.dma_start(skip_sb[:], skip.rearrange("(c q) -> q c", q=P))
 
         v_w = [keep.tile([P, S], U32, name="v_w%d" % g, align_bytes=64) for g in range(2)]
         v_sc = keep.tile([P, S], U8, align_bytes=64)
@@ -122,27 +120,28 @@ def tile_list_citation_chain_reader_kernel(
             nc.vector.tensor_copy(v_w[g][:], tab_w[g][:].bitcast(U32).indirect(offs_sb[:]))
 
         w1_bf, w1_q = {}, {}
-        first_picks = [keep.tile([P, (PACK + 1) * M], F32, name="picks%d" % g, align_bytes=64) for g in range(2)]
-        for g in range(2):
-            w1_bf[1, g] = first_picks[g][:, (PACK - 1) * M :].bitcast(BF16)
+        second_rebut = w1_raw[1][:, 4 * M : 8 * M]
+        first_gained = w1_raw[1][:, 5 * M : 7 * M].bitcast(BF16)
+        first_rebut = w1_raw[1][:, 7 * M : 11 * M]
+        first_quoted = keep.tile([P, PACK * M], F32, name="first_quoted", align_bytes=64)
 
-        def round_w1(a, g, c0, vector_share):
-            if c0 == 0 and a == 0:
+        def w1_views(a, g, c0):
+            if (a, g) not in w1_bf:
                 w1_bf[a, g] = keep.tile([P, PASS * PACK], BF16, name="w1_bf%d%d" % (a, g), align_bytes=64)
             src = w1_part[a, g, c0].rearrange("p j (m t) -> p m j t", t=PACK)
             dst = w1_bf[a, g][:].rearrange("p (t m j) -> p m j t", t=PACK, j=PACK)
-            dst = dst[:, c0 // PACK : c0 // PACK + src.shape[1]]
+            return dst[:, c0 // PACK : c0 // PACK + src.shape[1]], src
+
+        def round_w1(a, g, c0, vector_share):
+            dst, src = w1_views(a, g, c0)
             if vector_share > 0:
                 nc.vector.tensor_copy(dst[:, :vector_share], src[:, :vector_share])
-            if a == 1:
-                half = src.shape[1] // 2
-                for part in (slice(0, half), slice(half, 2 * half)):
-                    nc.gpsimd.tensor_scalar(
-                        dst[:, part].rearrange("p m j t -> p t m j"), src[:, part].rearrange("p m j t -> p t m j"),
-                        1.0, 0.0, ALU.mult, ALU.add,
-                    )
-            else:
-                nc.scalar.copy(dst[:, vector_share:], src[:, vector_share:])
+            nc.scalar.copy(dst[:, vector_share:], src[:, vector_share:])
+
+        def round_w1_gpsimd(a, g):
+            dst, src = w1_views(a, g, 0)
+            for t in range(PACK):
+                nc.gpsimd.tensor_scalar(dst[:, :, :, t], src[:, :, :, t], 1.0, 0.0, ALU.mult, ALU.add)
 
         def quantise(name, values, widths, tag=None):
             words = values.shape[1] // PACK
@@ -167,7 +166,7 @@ def tile_list_citation_chain_reader_kernel(
             codes, scales = w1_q[a, g]
             for half in range(2):
                 if g == 0:
-                    h_acc[a, t, half] = bank(2 * (t % 2) + half + (4 if a == 1 and t < 2 else 0), [P, BANK])
+                    h_acc[a, t, half] = bank(2 * t + half, [P, BANK])
                 cols = slice(half * BANK, (half + 1) * BANK)
                 nc.tensor.matmul_mx(
                     out=h_acc[a, t, half][:],
@@ -188,123 +187,123 @@ def tile_list_citation_chain_reader_kernel(
                 nc.scalar.copy(rows[:, BANK:], h_acc[a, t, 1][:])
             h[a, t] = rows
 
-        quoted, curved, rebut, x_q, b_q = {}, {}, {}, {}, {}
+        quoted, curved, rebut, x_bf, b_bf, x_q, b_q = {}, {}, {}, {}, {}, {}, {}
 
-        def open_quoted(a, m0, mc):
-            quoted[a, m0] = keep.tile([P, PACK, mc], F32, name="quoted", tag="quoted%d" % a)
+        def planes_tile(name, mc, tag):
+            return keep.tile([P, PACK, mc], F32, name=name, tag=tag, align_bytes=64)
 
-        def open_rebut(a, m0, mc, tag):
-            rebut[a, m0] = keep.tile([P, PACK, mc], F32, name="rebut", tag=tag, align_bytes=64)
-
-        def gather_quoted(a, m0, mc, t):
-            picks = pos1_sb[:, m0 // LIST_ROWS : (m0 + mc) // LIST_ROWS]
-            d = quoted[a, m0][:, t, :]
-            nc.vector.tensor_copy(d, h[a, t][:].indirect(picks))
+        def gather(dst, picks_sb, a, m0, mc, t):
+            picks = picks_sb[:, m0 // LIST_ROWS : (m0 + mc) // LIST_ROWS]
+            nc.vector.tensor_copy(dst, h[a, t][:].indirect(picks))
 
         def gelu(a, m0, t):
-            d = quoted[a, m0][:, t, :]
-            if a == 0 and t == 0:
-                curved[a, m0] = keep.tile([P, PACK, M], F32, name="curved", tag="w1_raw1")
-            if a == 1:
-                curved[a, m0] = quoted[a, m0]
-            nc.scalar.activation(curved[a, m0][:, t, :], d, ACT.Gelu_apprx_tanh, scale=tone_sb[:, a, t : t + 1])
+            nc.scalar.activation(
+                curved[a, m0][:, t, :], quoted[a, m0][t], ACT.Gelu_apprx_tanh, scale=tone_sb[:, a, t : t + 1]
+            )
 
-        def gather_rebut(a, m0, mc, t):
-            picks = pos2_sb[:, m0 // LIST_ROWS : (m0 + mc) // LIST_ROWS]
-            nc.vector.tensor_copy(rebut[a, m0][:, t, :], h[a, t][:].indirect(picks))
-
-        x_bf, b_bf = {}, {}
-
-        def woven(tile, mc):
+        def woven(tile):
             return tile[:].rearrange("p (c i t) -> p c t i", i=4, t=PACK)
 
         def planes(tile):
             return tile[:].rearrange("p t (c i) -> p c t i", i=4)
 
-        def round_x(a, m0, mc):
-            values = keep.tile([P, mc * PACK], BF16, name="x_bf", tag="x_bf%d_%d" % (a, m0), align_bytes=64)
-            factor = gain_sb[:, a, :PACK].unsqueeze(1).unsqueeze(3).to_broadcast([P, mc // 8, PACK, 4])
-            for part in (slice(0, mc // 8), slice(mc // 8, mc // 4)):
-                nc.vector.tensor_tensor(woven(values, mc)[:, part], planes(curved[a, m0])[:, part], factor, ALU.mult)
-            x_bf[a, m0] = values
+        gained = {}
 
-        def round_b(a, m0, mc, tag):
-            values = keep.tile([P, mc * PACK], BF16, name="b_bf", tag=tag, align_bytes=64)
-            nc.scalar.copy(woven(values, mc), planes(rebut[a, m0]))
-            b_bf[a, m0] = values
+        def bf16_tile(name, mc, tag):
+            return keep.tile([P, mc * PACK], BF16, name=name, tag=tag, align_bytes=64)
 
-        def quantise_x(a, m0, mc):
-            x_q[a, m0] = quantise("x%d_%d" % (a, m0), x_bf[a, m0], [mc // 2, mc // 2])
+        def apply_gain(a, m0, mc, t):
+            nc.gpsimd.tensor_scalar(
+                gained[a, m0][:, t, :], curved[a, m0][:, t, :],
+                gain_sb[:, a, t : t + 1], 0.0, ALU.mult, ALU.add,
+            )
 
-        def quantise_b(a, m0, mc):
-            b_q[a, m0] = quantise("b%d_%d" % (a, m0), b_bf[a, m0], [mc])
+        def weave(engine, dst, src, c0, c1):
+            if engine == "gpsimd":
+                for c in range(c0, c1, P):
+                    nc.gpsimd.tensor_scalar(
+                        dst[:, PACK * (c - c0) : PACK * (c - c0 + P)].rearrange("p (m t) -> p m t", t=PACK),
+                        src[:, :, c : c + P].rearrange("p t m -> p m t"),
+                        1.0, 0.0, ALU.mult, ALU.add,
+                    )
+                return
+            into = dst[:, : PACK * (c1 - c0)].rearrange("p (c i t) -> p c t i", i=4, t=PACK)
+            out_of = src[:, :, c0:c1].rearrange("p t (c i) -> p c t i", i=4)
+            if engine == "vector":
+                nc.vector.tensor_copy(into, out_of)
+            else:
+                nc.scalar.copy(into, out_of)
+
+        def quantise_x(a, m0, widths, tag=None):
+            x_q[a, m0] = quantise("x%d_%d" % (a, m0), x_bf[a, m0], widths, tag)
+
+        def quantise_b(a, m0, widths, tag=None):
+            b_q[a, m0] = quantise("b%d_%d" % (a, m0), b_bf[a, m0], widths, tag)
 
         y_acc = {}
 
-        def x_pass(a, piece_m0, mt, half):
-            c0 = mt * P - piece_m0
-            codes, scales = x_q[a, piece_m0]
-            if a == 0:
-                y_acc[mt, half] = bank((2 * mt + half + 4) % 8, [P, BANK])
-            n0 = half * BANK
-            nc.tensor.matmul_mx(
-                out=y_acc[mt, half][:],
-                lhsT=codes[:, c0 : c0 + P].bitcast(FP8X4),
-                lhsT_scale=scales[:, c0 : c0 + P],
-                rhs=w2_w[:, a, 2 * n0 : 2 * (n0 + BANK)].bitcast(FP4X4),
-                rhs_scale=w23_sc[:, a * H + n0 : a * H + n0 + BANK],
-                start=(a == 0),
-                stop=False,
-            )
-
-        def b_pass(a, piece_m0, mt, half):
-            c0 = mt * P - piece_m0
-            codes, scales = b_q[a, piece_m0]
-            n0 = half * BANK
-            nc.tensor.matmul_mx(
-                out=y_acc[mt, half][:],
-                lhsT=codes[:, c0 : c0 + P].bitcast(FP8X4),
-                lhsT_scale=scales[:, c0 : c0 + P],
-                rhs=w3_w[:, a, n0 : n0 + BANK].bitcast(FP8X4),
-                rhs_scale=w23_sc[4:P, a * H + n0 : a * H + n0 + BANK],
-                start=False,
-                stop=(a == 1),
-            )
-
-        turned = {}
-
-        def turn(m0, mc, half):
-            tiles = range(m0 // P, (m0 + mc) // P)
-            bent = {}
-            for mt in tiles:
-                bent[mt] = keep.tile([P, PACK, P], F32, name="bent", tag="bent%d%d" % (mt, half), align_bytes=64)
-                nc.scalar.activation(
-                    bent[mt][:].rearrange("m t p -> m p t"),
-                    y_acc[mt, half][:].rearrange("m (p t) -> m p t", t=PACK),
-                    ACT.Tanh,
+        def second_stage_passes(kind, a, m0, mc, piece_m0, last=False):
+            codes, scales = (x_q if kind == "x" else b_q)[a, piece_m0]
+            cols = slice(m0 - piece_m0, m0 - piece_m0 + mc)
+            for c in range(H // P):
+                pair, side = divmod(c, 2)
+                first = (m0, pair) not in y_acc
+                if first:
+                    y_acc[m0, pair] = bank(PACK * (m0 // mc) + pair, [P, 2, mc])
+                n0 = a * H + c * P
+                if kind == "x":
+                    weights = w2_w[:, a, 2 * c * P : 2 * (c + 1) * P].bitcast(FP4X4)
+                    weight_scales = w23_sc[:, n0 : n0 + P]
+                else:
+                    weights = w3_w[:, a, c * P : (c + 1) * P].bitcast(FP8X4)
+                    weight_scales = w23_sc[4:P, n0 : n0 + P]
+                nc.tensor.matmul_mx(
+                    out=y_acc[m0, pair][:, side, :],
+                    lhsT=weights,
+                    lhsT_scale=weight_scales,
+                    rhs=codes[:, cols].bitcast(FP8X4),
+                    rhs_scale=scales[:, cols],
+                    start=first,
+                    stop=(last and side == 1),
                 )
-            per_bank = PACK // len(tiles)
-            for number, mt_bank in enumerate(tiles):
-                target = bank((2 * mt_bank + half + 4) % 8, [P, per_bank, mc])
-                for u in range(per_bank):
-                    t = number * per_bank + u
-                    for mt in tiles:
-                        nc.tensor.transpose(target[:, u, mt * P - m0 : (mt + 1) * P - m0], bent[mt][:, t, :], ident[:])
-                    turned[m0, half, t] = target[:, u, :]
 
-        def finish(m0, mc, half, tag, per_store):
-            result = keep.tile([P, PACK, mc], F32, name="result", tag=tag, align_bytes=64)
-            piece_m0 = 0 if half == 0 else m0
-            c0 = m0 - piece_m0
-            rows = out[half * PASS : (half + 1) * PASS, m0 : m0 + mc].rearrange("(p t) m -> p t m", t=PACK)
-            for t in range(PACK):
+        residual = {}
+
+        def park(a, t0, t1):
+            rows = out[a * PASS : (a + 1) * PASS, :].rearrange("(p t) m -> p t m", t=PACK)
+            nc.sync.dma_start(rows[:, t0:t1, :], rebut[a, 0][:, t0:t1, :])
+
+        def fetch_residual(a, tag, parts):
+            rows = out[a * PASS : (a + 1) * PASS, :].rearrange("(c q) m -> q c m", q=P)
+            residual[a] = keep.tile([P, PACK, M], F32, name="residual", tag=tag, align_bytes=64)
+            step = M // parts
+            for c in range(0, M, step):
+                nc.sync.dma_start(residual[a][:, :, c : c + step], rows[:, :, c : c + step])
+
+        def finish(m0, mc, pair, singly):
+            bent = keep.tile([P, 2, mc], F32, name="bent", tag="bent%d_%d" % (m0, pair), align_bytes=64)
+            nc.scalar.activation(bent[:], y_acc[m0, pair][:], ACT.Tanh)
+            result = keep.tile([P, 2, mc], F32, name="result", tag="result%d_%d" % (m0, pair), align_bytes=64)
+            for side in range(2):
+                c = 2 * pair + side
                 nc.vector.scalar_tensor_tensor(
-                    result[:, t, :], rebut[half, piece_m0][:, t, c0 : c0 + mc], skip_sb[:, half, t : t + 1],
-                    turned[m0, half, t], ALU.mult, ALU.add,
+                    result[:, side, :], residual[c // PACK][:, c % PACK, m0 : m0 + mc], skip_sb[:, c : c + 1],
+                    bent[:, side, :], ALU.mult, ALU.add,
                 )
-                if (t + 1) % per_store == 0:
-                    done = slice(t + 1 - per_store, t + 1)
-                    nc.sync.dma_start(rows[:, done, :], result[:, done, :])
+                if singly:
+                    nc.sync.dma_start(out[c * P : (c + 1) * P, m0 : m0 + mc], result[:, side, :])
+            if not singly:
+                rows = out[2 * pair * P : 2 * (pair + 1) * P, m0 : m0 + mc]
+                nc.sync.dma_start(rows.rearrange("(c q) m -> q c m", q=P), result[:])
+
+        def round_x(a, m0, mc, tag):
+            x_bf[a, m0] = bf16_tile("x_bf", mc, tag)
+            factor = gain_sb[:, a, :PACK].unsqueeze(1).unsqueeze(3).to_broadcast([P, mc // 4, PACK, 4])
+            nc.vector.tensor_tensor(
+                x_bf[a, m0][:].rearrange("p (c i t) -> p c t i", i=4, t=PACK),
+                curved[a, m0][:].rearrange("p t (c i) -> p c t i", i=4),
+                factor, ALU.mult,
+            )
 
         gather_table(0)
         nc.vector.tensor_copy(v_sc[:], tab_sc[:].indirect(offs_sb[:]))
@@ -314,78 +313,87 @@ def tile_list_citation_chain_reader_kernel(
         round_w1(0, 1, 0, 0)
         round_w1(0, 1, PASS // 2, VECTOR_SHARE)
         quantise_w1(0, 1, [P] * PACK)
-        for t in range(PACK):
-            first_stage_pass(0, t, 0)
-            first_stage_pass(0, t, 1)
+        for g in range(2):
+            for t in range(PACK):
+                first_stage_pass(0, t, g)
         for t in range(PACK):
             fetch_h(0, t, vector_helps=(t == 0))
-        round_w1(1, 0, 0, 0)
+        round_w1_gpsimd(1, 0)
         round_w1(1, 1, 0, 0)
-        quoted[0, 0] = first_picks[0][:, : PACK * M].rearrange("p (t m) -> p t m", t=PACK)
-        rebut[0, 0] = first_picks[1][:, : PACK * M].rearrange("p (t m) -> p t m", t=PACK)
-        for t in range(PACK - 1):
-            gather_quoted(0, 0, M, t)
-            gather_rebut(0, 0, M, t)
+        quoted[0, 0] = [first_quoted[:, t * M : (t + 1) * M] for t in range(PACK)]
+        curved[0, 0] = planes_tile("curved", M, "w1_raw0")
+        rebut[0, 0] = first_rebut.rearrange("p (t m) -> p t m", t=PACK)
+        gather(quoted[0, 0][0], pos1_sb, 0, 0, M, 0)
+        gather(rebut[0, 0][:, 0, :], pos2_sb, 0, 0, M, 0)
+        for t in range(1, PACK - 1):
+            gather(quoted[0, 0][t], pos1_sb, 0, 0, M, t)
         quantise_w1(1, 0, [PASS])
-        gather_quoted(0, 0, M, PACK - 1)
+        gather(quoted[0, 0][PACK - 1], pos1_sb, 0, 0, M, PACK - 1)
         quantise_w1(1, 1, [PASS])
-        gather_rebut(0, 0, M, PACK - 1)
-        for t in range(PACK):
-            first_stage_pass(1, t, 0)
-            first_stage_pass(1, t, 1)
+        for t in range(1, PACK):
+            gather(rebut[0, 0][:, t, :], pos2_sb, 0, 0, M, t)
+        for g in range(2):
+            for t in range(PACK):
+                first_stage_pass(1, t, g)
+        park(0, 0, 1)
+        park(0, 1, PACK)
+        fetch_residual(0, "tab_w1", 1)
+        gained[0, 0] = first_gained.rearrange("p (t m) -> p t m", t=PACK)
         for t in range(PACK):
             gelu(0, 0, t)
-        round_x(0, 0, M)
-        quantise_x(0, 0, M)
+            apply_gain(0, 0, M, t)
         for t in range(PACK):
             fetch_h(1, t)
-        for mt in range(M // P):
-            for half in range(2):
-                x_pass(0, 0, mt, half)
-        round_b(0, 0, M, "b_bf0")
-
-        def last_passes(m0, mc):
-            for half in range(2):
-                for mt in range(m0 // P, (m0 + mc) // P):
-                    x_pass(1, m0, mt, half)
-                for mt in range(m0 // P, (m0 + mc) // P):
-                    b_pass(1, m0, mt, half)
-
         (m0, mc), (m1, md) = CHUNKS
-        open_quoted(1, m0, mc)
-        open_rebut(1, m0, mc, "rebut1")
+        x_bf[0, 0] = bf16_tile("x_bf", M, "x_bf0")
+        weave("gpsimd", x_bf[0, 0], gained[0, 0], 0, M)
+        quantise_x(0, 0, [M])
+        for m2, me in CHUNKS:
+            second_stage_passes("x", 0, m2, me, 0)
+        b_bf[0, 0] = bf16_tile("b_bf", M, "w1_raw0")
+        weave("scalar", b_bf[0, 0][:, : PACK * mc], rebut[0, 0], 0, mc)
+        weave("gpsimd", b_bf[0, 0][:, PACK * mc :], rebut[0, 0], mc, M)
+        quantise_b(0, 0, [M])
+        for m2, me in CHUNKS:
+            second_stage_passes("b", 0, m2, me, 0)
+
+        quoted_a = planes_tile("quoted", mc, "quoted_a")
+        quoted[1, m0] = [quoted_a[:, t, :] for t in range(PACK)]
+        rebut[1, 0] = second_rebut.rearrange("p (t m) -> p t m", t=PACK)
         for t in range(PACK):
-            gather_quoted(1, m0, mc, t)
-            gather_rebut(1, m0, mc, t)
-        quantise_b(0, 0, M)
-        for mt in range(M // P):
-            for half in range(2):
-                b_pass(0, 0, mt, half)
+            gather(rebut[1, 0][:, t, :], pos2_sb, 1, 0, M, t)
+            gather(quoted[1, m0][t], pos1_sb, 1, m0, mc, t)
+            park(1, t, t + 1)
+        fetch_residual(1, "tab_w0", 2)
+
+        shared = keep.tile([P, 6 * mc], F32, name="shared", align_bytes=64)
+        curved[1, m0] = planes_tile("curved", mc, "curved_a")
+        spread = shared[:].bitcast(BF16)[:, 4 * mc - mc // 2 : 12 * mc - mc // 2]
+        gained[1, m0] = spread.rearrange("p (t s) -> p t s", t=PACK)[:, :, :mc]
         for t in range(PACK):
             gelu(1, m0, t)
-        round_x(1, m0, mc)
-        round_b(1, m0, mc, "b_bf1")
-        quantise_x(1, m0, mc)
-        quantise_b(1, m0, mc)
-        last_passes(m0, mc)
+            apply_gain(1, m0, mc, t)
+        x_bf[1, m0] = bf16_tile("x_bf", mc, "x_bf_a")
+        weave("scalar", x_bf[1, m0], gained[1, m0], 0, mc)
+        quantise_x(1, m0, [mc])
+        second_stage_passes("x", 1, m0, mc, m0)
+        b_bf[1, m0] = shared[:, : 2 * mc].bitcast(BF16)
+        weave("scalar", b_bf[1, m0], rebut[1, 0], m0, m0 + mc)
+        b_bf[1, m1] = bf16_tile("b_bf", md, "quoted_a")
+        weave("gpsimd", b_bf[1, m1], rebut[1, 0], m1, m1 + md)
 
-        open_quoted(1, m1, md)
-        open_rebut(1, m1, md, "x_bf1_0")
+        quoted[1, m1] = [shared[:, (2 + t) * mc : (3 + t) * mc] for t in range(PACK)]
+        curved[1, m1] = planes_tile("curved", md, "x_bf_a")
         for t in range(PACK):
-            gather_quoted(1, m1, md, t)
-        for t in range(PACK):
-            gather_rebut(1, m1, md, t)
-        for t in range(PACK):
+            gather(quoted[1, m1][t], pos1_sb, 1, m1, md, t)
             gelu(1, m1, t)
-        for half in range(2):
-            turn(m0, mc, half)
-        round_x(1, m1, md)
-        round_b(1, m1, md, "bent11")
-        quantise_x(1, m1, md)
-        quantise_b(1, m1, md)
-        last_passes(m1, md)
-        finish(m0, mc, 0, "bent11", PACK)
-        finish(m0, mc, 1, "x_bf1_256", PACK)
-        for half in range(2):
-            turn(m1, md, half)
-            finish(m1, md, half, "result%d" % half, 2)
+        quantise_b(1, m0, [mc])
+        second_stage_passes("b", 1, m0, mc, m0, last=True)
+        quantise_b(1, m1, [md])
+        second_stage_passes("b", 1, m1, md, m1)
+        round_x(1, m1, md, "x_bf_b")
+        quantise_x(1, m1, [md])
+        second_stage_passes("x", 1, m1, md, m1, last=True)
+        for m2, me in CHUNKS:
+            for pair in range(PACK):
+                finish(m2, me, pair, m2 == m1 and pair == PACK - 1)

@@ -120,9 +120,9 @@ def tile_list_citation_chain_reader_kernel(
             nc.vector.tensor_copy(v_w[g][:], tab_w[g][:].bitcast(U32).indirect(offs_sb[:]))
 
         w1_bf, w1_q = {}, {}
-        second_rebut = w1_raw[1][:, 4 * M : 8 * M]
-        first_gained = w1_raw[1][:, 5 * M : 7 * M].bitcast(BF16)
-        first_rebut = w1_raw[1][:, 7 * M : 11 * M]
+        second_rebut = w1_raw[1][:, 2 * M : 6 * M]
+        first_rebut = w1_raw[1][:, 5 * M : 9 * M]
+        w1_bf[1, 0] = w1_raw[1][:, 6 * M : 8 * M].bitcast(BF16)
         first_quoted = keep.tile([P, PACK * M], F32, name="first_quoted", align_bytes=64)
 
         def w1_views(a, g, c0):
@@ -137,11 +137,6 @@ def tile_list_citation_chain_reader_kernel(
             if vector_share > 0:
                 nc.vector.tensor_copy(dst[:, :vector_share], src[:, :vector_share])
             nc.scalar.copy(dst[:, vector_share:], src[:, vector_share:])
-
-        def round_w1_gpsimd(a, g):
-            dst, src = w1_views(a, g, 0)
-            for t in range(PACK):
-                nc.gpsimd.tensor_scalar(dst[:, :, :, t], src[:, :, :, t], 1.0, 0.0, ALU.mult, ALU.add)
 
         def quantise(name, values, widths, tag=None):
             words = values.shape[1] // PACK
@@ -207,32 +202,12 @@ def tile_list_citation_chain_reader_kernel(
         def planes(tile):
             return tile[:].rearrange("p t (c i) -> p c t i", i=4)
 
-        gained = {}
-
         def bf16_tile(name, mc, tag):
             return keep.tile([P, mc * PACK], BF16, name=name, tag=tag, align_bytes=64)
 
-        def apply_gain(a, m0, mc, t):
-            nc.gpsimd.tensor_scalar(
-                gained[a, m0][:, t, :], curved[a, m0][:, t, :],
-                gain_sb[:, a, t : t + 1], 0.0, ALU.mult, ALU.add,
-            )
-
-        def weave(engine, dst, src, c0, c1):
-            if engine == "gpsimd":
-                for c in range(c0, c1, P):
-                    nc.gpsimd.tensor_scalar(
-                        dst[:, PACK * (c - c0) : PACK * (c - c0 + P)].rearrange("p (m t) -> p m t", t=PACK),
-                        src[:, :, c : c + P].rearrange("p t m -> p m t"),
-                        1.0, 0.0, ALU.mult, ALU.add,
-                    )
-                return
-            into = dst[:, : PACK * (c1 - c0)].rearrange("p (c i t) -> p c t i", i=4, t=PACK)
-            out_of = src[:, :, c0:c1].rearrange("p t (c i) -> p c t i", i=4)
-            if engine == "vector":
-                nc.vector.tensor_copy(into, out_of)
-            else:
-                nc.scalar.copy(into, out_of)
+        def weave(dst, src, c0, c1):
+            into = dst.rearrange("p (c i t) -> p c t i", i=4, t=PACK)
+            nc.scalar.copy(into, src[:, :, c0:c1].rearrange("p t (c i) -> p c t i", i=4))
 
         def quantise_x(a, m0, widths, tag=None):
             x_q[a, m0] = quantise("x%d_%d" % (a, m0), x_bf[a, m0], widths, tag)
@@ -318,19 +293,16 @@ def tile_list_citation_chain_reader_kernel(
                 first_stage_pass(0, t, g)
         for t in range(PACK):
             fetch_h(0, t, vector_helps=(t == 0))
-        round_w1_gpsimd(1, 0)
+        round_w1(1, 0, 0, 0)
         round_w1(1, 1, 0, 0)
         quoted[0, 0] = [first_quoted[:, t * M : (t + 1) * M] for t in range(PACK)]
         curved[0, 0] = planes_tile("curved", M, "w1_raw0")
         rebut[0, 0] = first_rebut.rearrange("p (t m) -> p t m", t=PACK)
-        gather(quoted[0, 0][0], pos1_sb, 0, 0, M, 0)
-        gather(rebut[0, 0][:, 0, :], pos2_sb, 0, 0, M, 0)
-        for t in range(1, PACK - 1):
-            gather(quoted[0, 0][t], pos1_sb, 0, 0, M, t)
         quantise_w1(1, 0, [PASS])
-        gather(quoted[0, 0][PACK - 1], pos1_sb, 0, 0, M, PACK - 1)
         quantise_w1(1, 1, [PASS])
-        for t in range(1, PACK):
+        for t in range(PACK):
+            gather(quoted[0, 0][t], pos1_sb, 0, 0, M, t)
+        for t in range(PACK):
             gather(rebut[0, 0][:, t, :], pos2_sb, 0, 0, M, t)
         for g in range(2):
             for t in range(PACK):
@@ -338,21 +310,17 @@ def tile_list_citation_chain_reader_kernel(
         park(0, 0, 1)
         park(0, 1, PACK)
         fetch_residual(0, "tab_w1", 1)
-        gained[0, 0] = first_gained.rearrange("p (t m) -> p t m", t=PACK)
         for t in range(PACK):
             gelu(0, 0, t)
-            apply_gain(0, 0, M, t)
+        round_x(0, 0, M, "x_bf0")
+        quantise_x(0, 0, [M])
         for t in range(PACK):
             fetch_h(1, t)
         (m0, mc), (m1, md) = CHUNKS
-        x_bf[0, 0] = bf16_tile("x_bf", M, "x_bf0")
-        weave("gpsimd", x_bf[0, 0], gained[0, 0], 0, M)
-        quantise_x(0, 0, [M])
         for m2, me in CHUNKS:
             second_stage_passes("x", 0, m2, me, 0)
         b_bf[0, 0] = bf16_tile("b_bf", M, "w1_raw0")
-        weave("scalar", b_bf[0, 0][:, : PACK * mc], rebut[0, 0], 0, mc)
-        weave("gpsimd", b_bf[0, 0][:, PACK * mc :], rebut[0, 0], mc, M)
+        weave(b_bf[0, 0][:], rebut[0, 0], 0, M)
         quantise_b(0, 0, [M])
         for m2, me in CHUNKS:
             second_stage_passes("b", 0, m2, me, 0)
@@ -366,31 +334,25 @@ def tile_list_citation_chain_reader_kernel(
             park(1, t, t + 1)
         fetch_residual(1, "tab_w0", 2)
 
-        shared = keep.tile([P, 6 * mc], F32, name="shared", align_bytes=64)
         curved[1, m0] = planes_tile("curved", mc, "curved_a")
-        spread = shared[:].bitcast(BF16)[:, 4 * mc - mc // 2 : 12 * mc - mc // 2]
-        gained[1, m0] = spread.rearrange("p (t s) -> p t s", t=PACK)[:, :, :mc]
         for t in range(PACK):
             gelu(1, m0, t)
-            apply_gain(1, m0, mc, t)
-        x_bf[1, m0] = bf16_tile("x_bf", mc, "x_bf_a")
-        weave("scalar", x_bf[1, m0], gained[1, m0], 0, mc)
+        round_x(1, m0, mc, "x_bf_a")
         quantise_x(1, m0, [mc])
         second_stage_passes("x", 1, m0, mc, m0)
-        b_bf[1, m0] = shared[:, : 2 * mc].bitcast(BF16)
-        weave("scalar", b_bf[1, m0], rebut[1, 0], m0, m0 + mc)
-        b_bf[1, m1] = bf16_tile("b_bf", md, "quoted_a")
-        weave("gpsimd", b_bf[1, m1], rebut[1, 0], m1, m1 + md)
+        b_bf[1, 0] = bf16_tile("b_bf", M, "b_bf1")
+        for m2, me in CHUNKS:
+            weave(b_bf[1, 0][:, PACK * m2 : PACK * (m2 + me)], rebut[1, 0], m2, m2 + me)
 
-        quoted[1, m1] = [shared[:, (2 + t) * mc : (3 + t) * mc] for t in range(PACK)]
-        curved[1, m1] = planes_tile("curved", md, "x_bf_a")
+        quoted_b = planes_tile("quoted", md, "curved_a")
+        quoted[1, m1] = [quoted_b[:, t, :] for t in range(PACK)]
+        curved[1, m1] = planes_tile("curved", md, "curved_b")
         for t in range(PACK):
             gather(quoted[1, m1][t], pos1_sb, 1, m1, md, t)
             gelu(1, m1, t)
-        quantise_b(1, m0, [mc])
-        second_stage_passes("b", 1, m0, mc, m0, last=True)
-        quantise_b(1, m1, [md])
-        second_stage_passes("b", 1, m1, md, m1)
+        quantise_b(1, 0, [M])
+        second_stage_passes("b", 1, m0, mc, 0, last=True)
+        second_stage_passes("b", 1, m1, md, 0)
         round_x(1, m1, md, "x_bf_b")
         quantise_x(1, m1, [md])
         second_stage_passes("x", 1, m1, md, m1, last=True)

@@ -83,10 +83,10 @@ def tile_list_citation_chain_reader_kernel(
         def load_factor(dst, vec):
             nc.sync.dma_start(dst[:, :, :PACK], vec.rearrange("(a p t) -> p a t", a=2, t=PACK))
 
-        load_table(0, 0, T // 2)
+        load_table(0, 0, T // 4)
         nc.sync.dma_start(offs_sb[:], offs)
-        load_table(0, T // 2, T)
         load_table_scales((0, 1))
+        load_table(0, T // 4, T)
         load_w1(0, 0, 1)
         load_table_scales((2, 3))
         load_table(1, 0, T)
@@ -255,21 +255,30 @@ def tile_list_citation_chain_reader_kernel(
             for c in range(0, M, step):
                 nc.sync.dma_start(residual[a][:, :, c : c + step], rows[:, :, c : c + step])
 
+        bent, result = {}, {}
+
+        def bend(m0, mc, pair):
+            if pair not in bent:
+                bent[pair] = keep.tile([P, 2, M], F32, name="bent", tag="bent%d" % pair, align_bytes=64)
+                result[pair] = keep.tile([P, 2, M], F32, name="result", tag="result%d" % pair, align_bytes=64)
+            nc.scalar.activation(bent[pair][:, :, m0 : m0 + mc], y_acc[m0, pair][:], ACT.Tanh)
+
         def finish(m0, mc, pair, singly):
-            bent = keep.tile([P, 2, mc], F32, name="bent", tag="bent%d_%d" % (m0, pair), align_bytes=64)
-            nc.scalar.activation(bent[:], y_acc[m0, pair][:], ACT.Tanh)
-            result = keep.tile([P, 2, mc], F32, name="result", tag="result%d_%d" % (m0, pair), align_bytes=64)
+            cols = slice(m0, m0 + mc)
             for side in range(2):
                 c = 2 * pair + side
                 nc.vector.scalar_tensor_tensor(
-                    result[:, side, :], residual[c // PACK][:, c % PACK, m0 : m0 + mc], skip_sb[:, c : c + 1],
-                    bent[:, side, :], ALU.mult, ALU.add,
+                    result[pair][:, side, cols], residual[c // PACK][:, c % PACK, cols], skip_sb[:, c : c + 1],
+                    bent[pair][:, side, cols], ALU.mult, ALU.add,
                 )
                 if singly:
-                    nc.sync.dma_start(out[c * P : (c + 1) * P, m0 : m0 + mc], result[:, side, :])
+                    nc.sync.dma_start(out[c * P : (c + 1) * P, cols], result[pair][:, side, cols])
             if not singly:
-                rows = out[2 * pair * P : 2 * (pair + 1) * P, m0 : m0 + mc]
-                nc.sync.dma_start(rows.rearrange("(c q) m -> q c m", q=P), result[:])
+                rows = out[2 * pair * P : 2 * (pair + 1) * P, cols]
+                nc.sync.dma_start(rows.rearrange("(c q) m -> q c m", q=P), result[pair][:, :, cols])
+
+        def apply_gain(dst, a, m0, t, c0, c1):
+            nc.scalar.activation(dst[:, t, :], curved[a, m0][:, t, c0:c1], ACT.Copy, scale=gain_sb[:, a, t : t + 1])
 
         def round_x(a, m0, mc, tag):
             x_bf[a, m0] = bf16_tile("x_bf", mc, tag)
@@ -335,14 +344,16 @@ def tile_list_citation_chain_reader_kernel(
         fetch_residual(1, "tab_w0", 2)
 
         curved[1, m0] = planes_tile("curved", mc, "curved_a")
+        gained = keep.tile([P, PACK, mc], BF16, name="gained", tag="gained", align_bytes=64)
         for t in range(PACK):
             gelu(1, m0, t)
-        round_x(1, m0, mc, "x_bf_a")
+            apply_gain(gained, 1, m0, t, 0, mc)
+        x_bf[1, m0] = bf16_tile("x_bf", mc, "x_bf_a")
+        weave(x_bf[1, m0][:], gained, 0, mc)
         quantise_x(1, m0, [mc])
         second_stage_passes("x", 1, m0, mc, m0)
-        b_bf[1, 0] = bf16_tile("b_bf", M, "b_bf1")
-        for m2, me in CHUNKS:
-            weave(b_bf[1, 0][:, PACK * m2 : PACK * (m2 + me)], rebut[1, 0], m2, m2 + me)
+        b_bf[1, m0] = bf16_tile("b_bf", mc, "gained")
+        weave(b_bf[1, m0][:], rebut[1, 0], m0, m0 + mc)
 
         quoted_b = planes_tile("quoted", md, "curved_a")
         quoted[1, m1] = [quoted_b[:, t, :] for t in range(PACK)]
@@ -350,12 +361,18 @@ def tile_list_citation_chain_reader_kernel(
         for t in range(PACK):
             gather(quoted[1, m1][t], pos1_sb, 1, m1, md, t)
             gelu(1, m1, t)
-        quantise_b(1, 0, [M])
-        second_stage_passes("b", 1, m0, mc, 0, last=True)
-        second_stage_passes("b", 1, m1, md, 0)
+        quantise_b(1, m0, [mc])
+        second_stage_passes("b", 1, m0, mc, m0, last=True)
+        b_bf[1, m1] = bf16_tile("b_bf", md, "curved_a")
+        weave(b_bf[1, m1][:], rebut[1, 0], m1, m1 + md)
         round_x(1, m1, md, "x_bf_b")
         quantise_x(1, m1, [md])
-        second_stage_passes("x", 1, m1, md, m1, last=True)
+        second_stage_passes("x", 1, m1, md, m1)
+        quantise_b(1, m1, [md])
+        second_stage_passes("b", 1, m1, md, m1, last=True)
+        for m2, me in CHUNKS:
+            for pair in range(PACK):
+                bend(m2, me, pair)
         for m2, me in CHUNKS:
             for pair in range(PACK):
                 finish(m2, me, pair, m2 == m1 and pair == PACK - 1)

@@ -60,10 +60,10 @@ def tile_list_citation_chain_reader_kernel(
 
         def load_w1(a, g, parts):
             if g == 0:
-                w1_raw[a] = keep.tile([P, 3 * PACK * PASS], F32, name="w1_raw", tag="w1_raw%d" % a, align_bytes=64)
+                w1_raw[a] = keep.tile([P, (8 + 6 * a) * M], F32, name="w1_raw", tag="w1_raw%d" % a, align_bytes=64)
             width = PASS // parts
             for c0 in range(0, PASS, width):
-                first = (2 * g * PASS + c0) * PACK
+                first = g * (4 + a) * M + c0 * PACK
                 part = w1_raw[a][:, first : first + PACK * width].rearrange("p (j c) -> p j c", j=PACK)
                 rows = w1[g * PASS : (g + 1) * PASS, a * PASS + c0 : a * PASS + c0 + width]
                 nc.sync.dma_start(part, rows.rearrange("(p j) c -> p j c", j=PACK))
@@ -120,14 +120,14 @@ def tile_list_citation_chain_reader_kernel(
             nc.vector.tensor_copy(v_w[g][:], tab_w[g][:].bitcast(U32).indirect(offs_sb[:]))
 
         w1_bf, w1_q = {}, {}
-        second_rebut = w1_raw[1][:, 2 * M : 6 * M]
-        first_rebut = w1_raw[1][:, 5 * M : 9 * M]
-        w1_bf[1, 0] = w1_raw[1][:, 6 * M : 8 * M].bitcast(BF16)
+        second_rebut = w1_raw[1][:, 9 * M : 13 * M]
+        first_rebut = w1_raw[1][:, 4 * M : 8 * M]
+        w1_bf[1, 1] = w1_raw[1][:, 12 * M :].bitcast(BF16)
         first_quoted = keep.tile([P, PACK * M], F32, name="first_quoted", align_bytes=64)
 
         def w1_views(a, g, c0):
             if (a, g) not in w1_bf:
-                w1_bf[a, g] = keep.tile([P, PASS * PACK], BF16, name="w1_bf%d%d" % (a, g), align_bytes=64)
+                w1_bf[a, g] = keep.tile([P, PASS * PACK], BF16, name="w1_bf", tag="w1_bf%d%d" % (a, g), align_bytes=64)
             src = w1_part[a, g, c0].rearrange("p j (m t) -> p m j t", t=PACK)
             dst = w1_bf[a, g][:].rearrange("p (t m j) -> p m j t", t=PACK, j=PACK)
             return dst[:, c0 // PACK : c0 // PACK + src.shape[1]], src
@@ -137,6 +137,11 @@ def tile_list_citation_chain_reader_kernel(
             if vector_share > 0:
                 nc.vector.tensor_copy(dst[:, :vector_share], src[:, :vector_share])
             nc.scalar.copy(dst[:, vector_share:], src[:, vector_share:])
+
+        def round_w1_gpsimd(a, g):
+            dst, src = w1_views(a, g, 0)
+            for t in range(PACK):
+                nc.gpsimd.tensor_scalar(dst[:, :, :, t], src[:, :, :, t], 1.0, 0.0, ALU.mult, ALU.add)
 
         def quantise(name, values, widths, tag=None):
             words = values.shape[1] // PACK
@@ -208,6 +213,14 @@ def tile_list_citation_chain_reader_kernel(
         def weave(dst, src, c0, c1):
             into = dst.rearrange("p (c i t) -> p c t i", i=4, t=PACK)
             nc.scalar.copy(into, src[:, :, c0:c1].rearrange("p t (c i) -> p c t i", i=4))
+
+        def weave_gpsimd(dst, src, c0, c1):
+            for c in range(c0, c1, P):
+                nc.gpsimd.tensor_scalar(
+                    dst[:, PACK * (c - c0) : PACK * (c - c0 + P)].rearrange("p (m t) -> p m t", t=PACK),
+                    src[:, :, c : c + P].rearrange("p t m -> p m t"),
+                    1.0, 0.0, ALU.mult, ALU.add,
+                )
 
         def quantise_x(a, m0, widths, tag=None):
             x_q[a, m0] = quantise("x%d_%d" % (a, m0), x_bf[a, m0], widths, tag)
@@ -302,7 +315,7 @@ def tile_list_citation_chain_reader_kernel(
                 first_stage_pass(0, t, g)
         for t in range(PACK):
             fetch_h(0, t, vector_helps=(t == 0))
-        round_w1(1, 0, 0, 0)
+        round_w1_gpsimd(1, 0)
         round_w1(1, 1, 0, 0)
         quoted[0, 0] = [first_quoted[:, t * M : (t + 1) * M] for t in range(PACK)]
         curved[0, 0] = planes_tile("curved", M, "w1_raw0")
@@ -316,23 +329,30 @@ def tile_list_citation_chain_reader_kernel(
         for g in range(2):
             for t in range(PACK):
                 first_stage_pass(1, t, g)
-        park(0, 0, 1)
-        park(0, 1, PACK)
+        park(0, 0, PACK)
         fetch_residual(0, "tab_w1", 1)
+        first_gained = w1_bf[1, 1].rearrange("p (t m) -> p t m", t=PACK)
         for t in range(PACK):
             gelu(0, 0, t)
-        round_x(0, 0, M, "x_bf0")
-        quantise_x(0, 0, [M])
+            nc.gpsimd.tensor_scalar(
+                first_gained[:, t, :], curved[0, 0][:, t, :], gain_sb[:, 0, t : t + 1], 0.0, ALU.mult, ALU.add
+            )
         for t in range(PACK):
             fetch_h(1, t)
         (m0, mc), (m1, md) = CHUNKS
+        b_bf[0, m0] = second_rebut[:, 2 * M : 3 * M].bitcast(BF16)
+        b_bf[0, m1] = bf16_tile("b_bf", md, "w1_11_codes")
+        for m2, me in CHUNKS:
+            weave_gpsimd(b_bf[0, m2], rebut[0, 0], m2, m2 + me)
+            quantise_b(0, m2, [me])
+            second_stage_passes("b", 0, m2, me, m2)
+
+        x_bf[0, 0] = bf16_tile("x_bf", M, "x_bf0")
+        weave(x_bf[0, 0][:], first_gained, 0, M)
+        quantise_x(0, 0, [M])
         for m2, me in CHUNKS:
             second_stage_passes("x", 0, m2, me, 0)
-        b_bf[0, 0] = bf16_tile("b_bf", M, "w1_raw0")
-        weave(b_bf[0, 0][:], rebut[0, 0], 0, M)
-        quantise_b(0, 0, [M])
-        for m2, me in CHUNKS:
-            second_stage_passes("b", 0, m2, me, 0)
+
 
         quoted_a = planes_tile("quoted", mc, "quoted_a")
         quoted[1, m0] = [quoted_a[:, t, :] for t in range(PACK)]
@@ -344,7 +364,8 @@ def tile_list_citation_chain_reader_kernel(
         fetch_residual(1, "tab_w0", 2)
 
         curved[1, m0] = planes_tile("curved", mc, "curved_a")
-        gained = keep.tile([P, PACK, mc], BF16, name="gained", tag="gained", align_bytes=64)
+        shared = keep.tile([P, 3 * mc], F32, name="shared", align_bytes=64)
+        gained = shared[:].bitcast(BF16)[:, 2 * mc :].rearrange("p (t m) -> p t m", t=PACK)
         for t in range(PACK):
             gelu(1, m0, t)
             apply_gain(gained, 1, m0, t, 0, mc)
@@ -352,24 +373,24 @@ def tile_list_citation_chain_reader_kernel(
         weave(x_bf[1, m0][:], gained, 0, mc)
         quantise_x(1, m0, [mc])
         second_stage_passes("x", 1, m0, mc, m0)
-        b_bf[1, m0] = bf16_tile("b_bf", mc, "gained")
-        weave(b_bf[1, m0][:], rebut[1, 0], m0, m0 + mc)
+        b_bf[1, m0] = bf16_tile("b_bf", mc, "w1_11_codes")
+        weave_gpsimd(b_bf[1, m0], rebut[1, 0], m0, m0 + mc)
+        b_bf[1, m1] = shared[:, : 2 * mc].bitcast(BF16)
+        weave(b_bf[1, m1], rebut[1, 0], m1, m1 + md)
 
-        quoted_b = planes_tile("quoted", md, "curved_a")
-        quoted[1, m1] = [quoted_b[:, t, :] for t in range(PACK)]
+        early = keep.tile([P, PACK - 1, md], F32, name="quoted", tag="curved_a", align_bytes=64)
+        quoted[1, m1] = [early[:, 0, :], early[:, 1, :], early[:, 2, :], shared[:, 2 * mc :]]
         curved[1, m1] = planes_tile("curved", md, "curved_b")
         for t in range(PACK):
             gather(quoted[1, m1][t], pos1_sb, 1, m1, md, t)
             gelu(1, m1, t)
-        quantise_b(1, m0, [mc])
+        quantise_b(1, m0, [mc], "x_bf_a")
         second_stage_passes("b", 1, m0, mc, m0, last=True)
-        b_bf[1, m1] = bf16_tile("b_bf", md, "curved_a")
-        weave(b_bf[1, m1][:], rebut[1, 0], m1, m1 + md)
+        quantise_b(1, m1, [md])
+        second_stage_passes("b", 1, m1, md, m1)
         round_x(1, m1, md, "x_bf_b")
         quantise_x(1, m1, [md])
-        second_stage_passes("x", 1, m1, md, m1)
-        quantise_b(1, m1, [md])
-        second_stage_passes("b", 1, m1, md, m1, last=True)
+        second_stage_passes("x", 1, m1, md, m1, last=True)
         for m2, me in CHUNKS:
             for pair in range(PACK):
                 bend(m2, me, pair)

@@ -23,7 +23,6 @@ BANK = 512
 LIST_ROWS = 16
 CHUNKS = ((0, 256), (256, 256))
 VECTOR_SHARE = 40
-CLEAR_SPLIT = 512
 
 
 def tile_list_citation_chain_reader_kernel(
@@ -44,8 +43,7 @@ def tile_list_citation_chain_reader_kernel(
         pos2_sb = lists.tile([P, M // LIST_ROWS], U16)
 
         tab_sc = keep.tile([P, T], U8, tag="tab_sc", align_bytes=64)
-        nc.gpsimd.memset(tab_sc[:].bitcast(I32)[:, :CLEAR_SPLIT], 0)
-        nc.vector.memset(tab_sc[:].bitcast(I32)[:, CLEAR_SPLIT:], 0)
+        nc.vector.memset(tab_sc[:].bitcast(I32), 0)
 
         warm = keep.tile([P, 8], F32)
         nc.vector.memset(warm[:], 0.0)
@@ -166,7 +164,7 @@ def tile_list_citation_chain_reader_kernel(
             codes, scales = w1_q[a, g]
             for half in range(2):
                 if g == 0:
-                    h_acc[a, t, half] = bank(2 * t + half, [P, BANK])
+                    h_acc[a, t, half] = bank(2 * (t % (PACK // (a + 1))) + half, [P, BANK])
                 cols = slice(half * BANK, (half + 1) * BANK)
                 nc.tensor.matmul_mx(
                     out=h_acc[a, t, half][:],

@@ -22,7 +22,7 @@ PASS = P * PACK
 BANK = 512
 LIST_ROWS = 16
 CHUNKS = ((0, 256), (256, 256))
-VECTOR_SHARE = 40
+H_BANKS = (((0, 1, 2, 3), (4, 5), (6, 7), (0, 1)), ((0, 1), (2, 3), (0, 1), (2, 3)))
 
 
 def tile_list_citation_chain_reader_kernel(
@@ -130,11 +130,8 @@ def tile_list_citation_chain_reader_kernel(
             dst = w1_bf[a, g][:].rearrange("p (t m j) -> p m j t", t=PACK, j=PACK)
             return dst[:, c0 // PACK : c0 // PACK + src.shape[1]], src
 
-        def round_w1(a, g, c0, vector_share):
-            dst, src = w1_views(a, g, c0)
-            if vector_share > 0:
-                nc.vector.tensor_copy(dst[:, :vector_share], src[:, :vector_share])
-            nc.scalar.copy(dst[:, vector_share:], src[:, vector_share:])
+        def round_w1(a, g, c0):
+            nc.scalar.copy(*w1_views(a, g, c0))
 
         def round_w1_gpsimd(a, g):
             dst, src = w1_views(a, g, 0)
@@ -162,10 +159,12 @@ def tile_list_citation_chain_reader_kernel(
 
         def first_stage_pass(a, t, g):
             codes, scales = w1_q[a, g]
-            for half in range(2):
+            banks = H_BANKS[a][t]
+            width = S // len(banks)
+            for half, number in enumerate(banks):
                 if g == 0:
-                    h_acc[a, t, half] = bank(2 * (t % (PACK // (a + 1))) + half, [P, BANK])
-                cols = slice(half * BANK, (half + 1) * BANK)
+                    h_acc[a, t, half] = bank(number, [P, width])
+                cols = slice(half * width, (half + 1) * width)
                 nc.tensor.matmul_mx(
                     out=h_acc[a, t, half][:],
                     lhsT=codes[:, t * P : (t + 1) * P].bitcast(FP8X4),
@@ -178,11 +177,12 @@ def tile_list_citation_chain_reader_kernel(
 
         def fetch_h(a, t, vector_helps=False):
             rows = keep.tile([P, S], F32, name="h", tag="h%d%d" % (a, t), align_bytes=64)
-            nc.scalar.copy(rows[:, :BANK], h_acc[a, t, 0][:])
-            if vector_helps:
-                nc.vector.tensor_copy(rows[:, BANK:], h_acc[a, t, 1][:])
-            else:
-                nc.scalar.copy(rows[:, BANK:], h_acc[a, t, 1][:])
+            width = S // len(H_BANKS[a][t])
+            for half in range(len(H_BANKS[a][t])):
+                if vector_helps and half % 2:
+                    nc.vector.tensor_copy(rows[:, half * width : (half + 1) * width], h_acc[a, t, half][:])
+                else:
+                    nc.scalar.copy(rows[:, half * width : (half + 1) * width], h_acc[a, t, half][:])
             h[a, t] = rows
 
         quoted, curved, rebut, x_bf, b_bf, x_q, b_q = {}, {}, {}, {}, {}, {}, {}
@@ -302,19 +302,24 @@ def tile_list_citation_chain_reader_kernel(
 
         gather_table(0)
         nc.vector.tensor_copy(v_sc[:], tab_sc[:].indirect(offs_sb[:]))
-        round_w1(0, 0, 0, 0)
+        round_w1(0, 0, 0)
         quantise_w1(0, 0, [PASS], "tab_sc")
         gather_table(1)
-        round_w1(0, 1, 0, 0)
-        round_w1(0, 1, PASS // 2, VECTOR_SHARE)
+        round_w1(0, 1, 0)
+        dst, src = w1_views(0, 1, PASS // 2)
+        nc.vector.tensor_copy(dst[:, :, :, 0], src[:, :, :, 0])
+        nc.scalar.copy(dst[:, :, :, 1:], src[:, :, :, 1:])
         quantise_w1(0, 1, [P] * PACK)
         for g in range(2):
-            for t in range(PACK):
+            for t in range(PACK - 1):
                 first_stage_pass(0, t, g)
-        for t in range(PACK):
-            fetch_h(0, t, vector_helps=(t == 0))
+        fetch_h(0, 0, vector_helps=True)
+        for g in range(2):
+            first_stage_pass(0, PACK - 1, g)
+        for t in range(1, PACK):
+            fetch_h(0, t)
         round_w1_gpsimd(1, 0)
-        round_w1(1, 1, 0, 0)
+        round_w1(1, 1, 0)
         quoted[0, 0] = [first_quoted[:, t * M : (t + 1) * M] for t in range(PACK)]
         curved[0, 0] = planes_tile("curved", M, "w1_raw0")
         rebut[0, 0] = first_rebut.rearrange("p (t m) -> p t m", t=PACK)

@@ -58,7 +58,7 @@ def tile_list_citation_chain_reader_kernel(
 
         def load_w1(a, g, parts):
             if g == 0:
-                w1_raw[a] = keep.tile([P, (8 + 6 * a) * M], F32, name="w1_raw", tag="w1_raw%d" % a, align_bytes=64)
+                w1_raw[a] = keep.tile([P, (8 + 7 * a) * M], F32, name="w1_raw", tag="w1_raw%d" % a, align_bytes=64)
             width = PASS // parts
             for c0 in range(0, PASS, width):
                 first = g * (4 + a) * M + c0 * PACK
@@ -81,6 +81,16 @@ def tile_list_citation_chain_reader_kernel(
         def load_factor(dst, vec):
             nc.sync.dma_start(dst[:, :, :PACK], vec.rearrange("(a p t) -> p a t", a=2, t=PACK))
 
+        w23_sc = keep.tile([P, 2 * H], U8, align_bytes=64)
+        nc.vector.memset(w23_sc[:].bitcast(I32), 0)
+
+        def load_weight_scales(first, rows):
+            for r in range(4):
+                nc.sync.dma_start(
+                    w23_sc[first + r : P : 32, :].bitcast(I32).rearrange("q (a n) -> q a n", a=2),
+                    rows[:, r:16:4, :].rearrange("a q n -> q a n").bitcast(I32),
+                )
+
         load_table(0, 0, T // 4)
         nc.sync.dma_start(offs_sb[:], offs)
         load_table_scales((0, 1))
@@ -92,22 +102,15 @@ def tile_list_citation_chain_reader_kernel(
         nc.sync.dma_start(pos1_sb[:], pos1)
         nc.sync.dma_start(pos2_sb[:], pos2)
         load_w1(1, 0, 1)
+        load_weight_scales(0, w2_scales)
         load_w1(1, 1, 1)
         load_factor(tone_sb, tone)
         load_factor(gain_sb, gain)
+        load_weight_scales(4, w3_scales)
         w2_w = keep.tile([P, 2, 2 * H], U8, align_bytes=64)
         nc.sync.dma_start(w2_w[:].bitcast(I32), w2_words.rearrange("a p n -> p a n").bitcast(I32))
         w3_w = keep.tile([P, 2, H], I32, align_bytes=64)
         nc.sync.dma_start(w3_w[:], w3_words.rearrange("a p n i -> p a (n i)").bitcast(I32))
-        w23_sc = keep.tile([P, 2 * H], U8, align_bytes=64)
-        nc.vector.memset(w23_sc[:].bitcast(I32), 0)
-        for r in range(4):
-            for first, rows in ((0, w2_scales), (4, w3_scales)):
-                nc.sync.dma_start(
-                    w23_sc[first + r : P : 32, :].bitcast(I32).rearrange("q (a n) -> q a n", a=2),
-                    rows[:, r:16:4, :].rearrange("a q n -> q a n").bitcast(I32),
-                )
-
         with nc.allow_non_contiguous_dma(reason="one factor for each partition and row tile"):
             nc.sync.dma_start(skip_sb[:], skip.rearrange("(c q) -> q c", q=P))
 
@@ -120,8 +123,9 @@ def tile_list_citation_chain_reader_kernel(
         w1_bf, w1_q = {}, {}
         second_rebut = w1_raw[1][:, 9 * M : 13 * M]
         first_rebut = w1_raw[1][:, 4 * M : 8 * M]
-        w1_bf[1, 1] = w1_raw[1][:, 12 * M :].bitcast(BF16)
-        first_quoted = keep.tile([P, PACK * M], F32, name="first_quoted", align_bytes=64)
+        w1_bf[1, 0] = w1_raw[1][:, 13 * M :].bitcast(BF16)
+        w1_bf[1, 1] = w1_raw[1][:, 12 * M : 14 * M].bitcast(BF16)
+        first_quoted = keep.tile([P, 2 * M], F32, name="first_quoted", align_bytes=64)
 
         def w1_views(a, g, c0):
             if (a, g) not in w1_bf:
@@ -133,10 +137,10 @@ def tile_list_citation_chain_reader_kernel(
         def round_w1(a, g, c0):
             nc.scalar.copy(*w1_views(a, g, c0))
 
-        def round_w1_gpsimd(a, g):
-            dst, src = w1_views(a, g, 0)
-            for t in range(PACK):
-                nc.gpsimd.tensor_scalar(dst[:, :, :, t], src[:, :, :, t], 1.0, 0.0, ALU.mult, ALU.add)
+        def round_w1_gpsimd(a, g, t0, step):
+            dst, src = (view[:, :, :, t0:].rearrange("p m j t -> p m t j") for view in w1_views(a, g, 0))
+            for m2 in range(0, P, step):
+                nc.gpsimd.tensor_scalar(dst[:, m2 : m2 + step], src[:, m2 : m2 + step], 1.0, 0.0, ALU.mult, ALU.add)
 
         def quantise(name, values, widths, tag=None):
             words = values.shape[1] // PACK
@@ -255,9 +259,9 @@ def tile_list_citation_chain_reader_kernel(
 
         residual = {}
 
-        def park(a, t0, t1):
+        def park(a, t, m0, mc):
             rows = out[a * PASS : (a + 1) * PASS, :].rearrange("(p t) m -> p t m", t=PACK)
-            nc.sync.dma_start(rows[:, t0:t1, :], rebut[a, 0][:, t0:t1, :])
+            nc.sync.dma_start(rows[:, t, m0 : m0 + mc], rebut[a, 0][:, t, m0 : m0 + mc])
 
         def fetch_residual(a, tag, parts):
             rows = out[a * PASS : (a + 1) * PASS, :].rearrange("(c q) m -> q c m", q=P)
@@ -271,22 +275,25 @@ def tile_list_citation_chain_reader_kernel(
         def bend(m0, mc, pair):
             if pair not in bent:
                 bent[pair] = keep.tile([P, 2, M], F32, name="bent", tag="bent%d" % pair, align_bytes=64)
-                result[pair] = keep.tile([P, 2, M], F32, name="result", tag="result%d" % pair, align_bytes=64)
             nc.scalar.activation(bent[pair][:, :, m0 : m0 + mc], y_acc[m0, pair][:], ACT.Tanh)
 
         def finish(m0, mc, pair, singly):
             cols = slice(m0, m0 + mc)
+            if m0 == 0:
+                result[m0, pair] = keep.tile([P, 2, mc], F32, name="result", tag="result%d" % pair, align_bytes=64)[:]
+            else:
+                result[m0, pair] = bent[(pair + 2) % PACK][:, :, :mc]
             for side in range(2):
                 c = 2 * pair + side
                 nc.vector.scalar_tensor_tensor(
-                    result[pair][:, side, cols], residual[c // PACK][:, c % PACK, cols], skip_sb[:, c : c + 1],
+                    result[m0, pair][:, side, :], residual[c // PACK][:, c % PACK, cols], skip_sb[:, c : c + 1],
                     bent[pair][:, side, cols], ALU.mult, ALU.add,
                 )
                 if singly:
-                    nc.sync.dma_start(out[c * P : (c + 1) * P, cols], result[pair][:, side, cols])
+                    nc.sync.dma_start(out[c * P : (c + 1) * P, cols], result[m0, pair][:, side, :])
             if not singly:
                 rows = out[2 * pair * P : 2 * (pair + 1) * P, cols]
-                nc.sync.dma_start(rows.rearrange("(c q) m -> q c m", q=P), result[pair][:, :, cols])
+                nc.sync.dma_start(rows.rearrange("(c q) m -> q c m", q=P), result[m0, pair])
 
         def apply_gain(dst, a, m0, t, c0, c1):
             nc.scalar.activation(dst[:, t, :], curved[a, m0][:, t, c0:c1], ACT.Copy, scale=gain_sb[:, a, t : t + 1])
@@ -318,21 +325,23 @@ def tile_list_citation_chain_reader_kernel(
             first_stage_pass(0, PACK - 1, g)
         for t in range(1, PACK):
             fetch_h(0, t)
-        round_w1_gpsimd(1, 0)
-        round_w1(1, 1, 0)
-        quoted[0, 0] = [first_quoted[:, t * M : (t + 1) * M] for t in range(PACK)]
+        round_w1_gpsimd(1, 0, 0, P // 4)
+        quantise_w1(1, 0, [PASS])
+        dst, src = w1_views(1, 1, 0)
+        nc.scalar.copy(dst[:, :, :, :2], src[:, :, :, :2])
+        round_w1_gpsimd(1, 1, 2, P // 2)
+        quoted[0, 0] = [rows[:, t * M : (t + 1) * M] for rows in (first_quoted, w1_raw[1]) for t in range(2)]
         curved[0, 0] = planes_tile("curved", M, "w1_raw0")
         rebut[0, 0] = first_rebut.rearrange("p (t m) -> p t m", t=PACK)
-        quantise_w1(1, 0, [PASS])
         quantise_w1(1, 1, [PASS])
         for t in range(PACK):
             gather(quoted[0, 0][t], pos1_sb, 0, 0, M, t)
         for t in range(PACK):
             gather(rebut[0, 0][:, t, :], pos2_sb, 0, 0, M, t)
+            park(0, t, 0, M)
         for g in range(2):
             for t in range(PACK):
                 first_stage_pass(1, t, g)
-        park(0, 0, PACK)
         fetch_residual(0, "tab_w1", 1)
         first_gained = w1_bf[1, 1].rearrange("p (t m) -> p t m", t=PACK)
         for t in range(PACK):
@@ -360,10 +369,14 @@ def tile_list_citation_chain_reader_kernel(
         quoted_a = planes_tile("quoted", mc, "quoted_a")
         quoted[1, m0] = [quoted_a[:, t, :] for t in range(PACK)]
         rebut[1, 0] = second_rebut.rearrange("p (t m) -> p t m", t=PACK)
-        for t in range(PACK):
+        for t in range(PACK - 1):
             gather(rebut[1, 0][:, t, :], pos2_sb, 1, 0, M, t)
             gather(quoted[1, m0][t], pos1_sb, 1, m0, mc, t)
-            park(1, t, t + 1)
+            park(1, t, 0, M)
+        gather(quoted[1, m0][3], pos1_sb, 1, m0, mc, 3)
+        for m2, me in CHUNKS:
+            gather(rebut[1, 0][:, 3, m2 : m2 + me], pos2_sb, 1, m2, me, 3)
+            park(1, 3, m2, me)
         fetch_residual(1, "tab_w0", 2)
 
         curved[1, m0] = planes_tile("curved", mc, "curved_a")

@@ -352,11 +352,10 @@ def tile_list_citation_chain_reader_kernel(
         for t in range(PACK):
             fetch_h(1, t)
         (m0, mc), (m1, md) = CHUNKS
-        b_bf[0, m0] = second_rebut[:, 2 * M : 3 * M].bitcast(BF16)
-        b_bf[0, m1] = bf16_tile("b_bf", md, "w1_11_codes")
         for m2, me in CHUNKS:
+            b_bf[0, m2] = bf16_tile("b_bf", me, "b_lower")
             weave_gpsimd(b_bf[0, m2], rebut[0, 0], m2, m2 + me)
-            quantise_b(0, m2, [me])
+            quantise_b(0, m2, [me], "w1_10_codes" if m2 == m0 else None)
             second_stage_passes("b", 0, m2, me, m2)
 
         x_bf[0, 0] = bf16_tile("x_bf", M, "x_bf0")

@@ -58,10 +58,10 @@ def tile_list_citation_chain_reader_kernel(
 
         def load_w1(a, g, parts):
             if g == 0:
-                w1_raw[a] = keep.tile([P, (8 + 7 * a) * M], F32, name="w1_raw", tag="w1_raw%d" % a, align_bytes=64)
+                w1_raw[a] = keep.tile([P, (8 + 8 * a) * M], F32, name="w1_raw", tag="w1_raw%d" % a, align_bytes=64)
             width = PASS // parts
             for c0 in range(0, PASS, width):
-                first = g * (4 + a) * M + c0 * PACK
+                first = (a + g * (4 + a)) * M + c0 * PACK
                 part = w1_raw[a][:, first : first + PACK * width].rearrange("p (j c) -> p j c", j=PACK)
                 rows = w1[g * PASS : (g + 1) * PASS, a * PASS + c0 : a * PASS + c0 + width]
                 nc.sync.dma_start(part, rows.rearrange("(p j) c -> p j c", j=PACK))
@@ -121,10 +121,10 @@ def tile_list_citation_chain_reader_kernel(
             nc.vector.tensor_copy(v_w[g][:], tab_w[g][:].bitcast(U32).indirect(offs_sb[:]))
 
         w1_bf, w1_q = {}, {}
-        second_rebut = w1_raw[1][:, 9 * M : 13 * M]
-        first_rebut = w1_raw[1][:, 4 * M : 8 * M]
-        w1_bf[1, 0] = w1_raw[1][:, 13 * M :].bitcast(BF16)
-        w1_bf[1, 1] = w1_raw[1][:, 12 * M : 14 * M].bitcast(BF16)
+        second_rebut = w1_raw[1][:, 10 * M : 14 * M]
+        first_rebut = w1_raw[1][:, : 12 * M]
+        w1_bf[1, 0] = w1_raw[1][:, 14 * M :].bitcast(BF16)
+        w1_bf[1, 1] = w1_raw[1][:, 13 * M : 15 * M].bitcast(BF16)
         first_quoted = keep.tile([P, 2 * M], F32, name="first_quoted", align_bytes=64)
 
         def w1_views(a, g, c0):
@@ -330,9 +330,9 @@ def tile_list_citation_chain_reader_kernel(
         dst, src = w1_views(1, 1, 0)
         nc.scalar.copy(dst[:, :, :, :2], src[:, :, :, :2])
         round_w1_gpsimd(1, 1, 2, P // 2)
-        quoted[0, 0] = [rows[:, t * M : (t + 1) * M] for rows in (first_quoted, w1_raw[1]) for t in range(2)]
+        quoted[0, 0] = [rows[:, t * M : (t + 1) * M] for rows in (first_quoted, w1_raw[1][:, M:]) for t in range(2)]
         curved[0, 0] = planes_tile("curved", M, "w1_raw0")
-        rebut[0, 0] = first_rebut.rearrange("p (t m) -> p t m", t=PACK)
+        rebut[0, 0] = first_rebut.rearrange("p (t m) -> p t m", t=PACK)[:, :, :M]
         quantise_w1(1, 1, [PASS])
         for t in range(PACK):
             gather(quoted[0, 0][t], pos1_sb, 0, 0, M, t)

@@ -22,7 +22,7 @@ PASS = P * PACK
 BANK = 512
 LIST_ROWS = 16
 CHUNKS = ((0, 256), (256, 256))
-H_BANKS = (((0, 1, 2, 3), (4, 5), (6, 7), (0, 1)), ((0, 1), (2, 3), (0, 1), (2, 3)))
+H_BANKS = (((0, 1, 2, 3), (4, 5), (6, 7), (4, 5)), ((0, 1), (2, 3), (0, 1), (2, 3)))
 
 
 def tile_list_citation_chain_reader_kernel(
@@ -32,6 +32,7 @@ def tile_list_citation_chain_reader_kernel(
     nc = tc.nc
     with ExitStack() as ctx:
         lists = ctx.enter_context(tc.tile_pool(name="lists", bufs=1))
+        staged = ctx.enter_context(tc.tile_pool(name="staged", bufs=1))
         keep = ctx.enter_context(tc.tile_pool(name="keep", bufs=1))
         psum = ctx.enter_context(tc.psum_pool(name="psum", bufs=1))
 
@@ -42,89 +43,82 @@ def tile_list_citation_chain_reader_kernel(
         pos1_sb = lists.tile([P, M // LIST_ROWS], U16)
         pos2_sb = lists.tile([P, M // LIST_ROWS], U16)
 
-        tab_sc = keep.tile([P, T], U8, tag="tab_sc", align_bytes=64)
+        def stage(name, shape, dtype, offset):
+            return staged.tile(shape, dtype, name=name, offset=offset, align_bytes=64)
+
+        tab_sc = stage("tab_sc", [P, T], U8, 4 * T - 64)
         nc.vector.memset(tab_sc[:].bitcast(I32), 0)
 
         warm = keep.tile([P, 8], F32)
         nc.vector.memset(warm[:], 0.0)
         nc.scalar.activation(warm[:], warm[:], ACT.Gelu_apprx_tanh)
 
-        tab_w = [keep.tile([P, T], I32, name="tab_w", tag="tab_w%d" % g, align_bytes=64) for g in range(2)]
+        first_at = 5 * T - 128 + 16 * PASS
+        tab_w = [stage("tab_w", [P, T], I32, first_at)]
         w1_raw, w1_part = {}, {}
 
         def load_table(g, c0, c1):
             words = tab_words[g].rearrange("p n i -> p (n i)").bitcast(I32)
             nc.sync.dma_start(tab_w[g][:, c0:c1], words[:, c0:c1])
 
-        def load_w1(a, g, parts):
-            if g == 0:
-                w1_raw[a] = keep.tile([P, (8 + 8 * a) * M], F32, name="w1_raw", tag="w1_raw%d" % a, align_bytes=64)
+        def load_w1(a, g, raw, parts):
             width = PASS // parts
             for c0 in range(0, PASS, width):
-                first = (a + g * (4 + a)) * M + c0 * PACK
-                part = w1_raw[a][:, first : first + PACK * width].rearrange("p (j c) -> p j c", j=PACK)
+                part = raw[:, c0 * PACK : (c0 + width) * PACK].rearrange("p (j c) -> p j c", j=PACK)
                 rows = w1[g * PASS : (g + 1) * PASS, a * PASS + c0 : a * PASS + c0 + width]
                 nc.sync.dma_start(part, rows.rearrange("(p j) c -> p j c", j=PACK))
                 w1_part[a, g, c0] = part
 
-        tone_sb = keep.tile([P, 2, 2 * PACK], F32)
-        gain_sb = keep.tile([P, 2, 2 * PACK], F32)
-        skip_sb = keep.tile([P, H // P], F32)
-
-        def load_table_scales(rows):
-            for r in rows:
-                for g in range(2):
-                    nc.sync.dma_start(
-                        tab_sc[4 * g + r : P : 32, :].bitcast(I32), tab_scales[g, r:16:4, :].bitcast(I32)
-                    )
-
         def load_factor(dst, vec):
             nc.sync.dma_start(dst[:, :, :PACK], vec.rearrange("(a p t) -> p a t", a=2, t=PACK))
 
-        w23_sc = keep.tile([P, 2 * H], U8, align_bytes=64)
-        nc.vector.memset(w23_sc[:].bitcast(I32), 0)
-
-        def load_weight_scales(first, rows):
-            for r in range(4):
-                nc.sync.dma_start(
-                    w23_sc[first + r : P : 32, :].bitcast(I32).rearrange("q (a n) -> q a n", a=2),
-                    rows[:, r:16:4, :].rearrange("a q n -> q a n").bitcast(I32),
-                )
-
         load_table(0, 0, T // 4)
         nc.sync.dma_start(offs_sb[:], offs)
-        load_table_scales((0, 1))
-        load_table(0, T // 4, T)
-        load_w1(0, 0, 1)
-        load_table_scales((2, 3))
-        load_table(1, 0, T)
-        load_w1(0, 1, 2)
         nc.sync.dma_start(pos1_sb[:], pos1)
         nc.sync.dma_start(pos2_sb[:], pos2)
-        load_w1(1, 0, 1)
-        load_weight_scales(0, w2_scales)
-        load_w1(1, 1, 1)
-        load_factor(tone_sb, tone)
-        load_factor(gain_sb, gain)
-        load_weight_scales(4, w3_scales)
-        w2_w = keep.tile([P, 2, 2 * H], U8, align_bytes=64)
-        nc.sync.dma_start(w2_w[:].bitcast(I32), w2_words.rearrange("a p n -> p a n").bitcast(I32))
-        w3_w = keep.tile([P, 2, H], I32, align_bytes=64)
-        nc.sync.dma_start(w3_w[:], w3_words.rearrange("a p n i -> p a (n i)").bitcast(I32))
-        with nc.allow_non_contiguous_dma(reason="one factor for each partition and row tile"):
-            nc.sync.dma_start(skip_sb[:], skip.rearrange("(c q) -> q c", q=P))
+        nc.sync.dma_start(tab_sc[0:P:4, :].bitcast(I32), tab_scales.rearrange("g q n -> (g q) n").bitcast(I32))
+        load_table(0, T // 4, T)
+        w1_raw[0] = keep.tile([P, PACK * PASS], F32, name="w1_raw", tag="w1_raw0", align_bytes=64)
+        load_w1(0, 0, w1_raw[0][:], 1)
 
         v_w = [keep.tile([P, S], U32, name="v_w%d" % g, align_bytes=64) for g in range(2)]
         v_sc = keep.tile([P, S], U8, align_bytes=64)
+        nc.vector.memset(v_sc[:].bitcast(I32), 0)
+        v_spread = keep.tile([P, S], U8, align_bytes=64)
+        nc.vector.tensor_copy(v_spread[:], tab_sc[:].indirect(offs_sb[:]))
+
+        def deal_table_scales(g):
+            for r in range(4):
+                nc.sync.dma_start(
+                    v_sc[4 * g + r : P : 32, :].bitcast(I32),
+                    v_spread[64 * g + 4 * r : 64 * (g + 1) : 16, :].bitcast(I32),
+                )
 
         def gather_table(g):
             nc.vector.tensor_copy(v_w[g][:], tab_w[g][:].bitcast(U32).indirect(offs_sb[:]))
 
+        gather_table(0)
+        deal_table_scales(0)
+        tab_w.append(stage("tab_w", [P, T], I32, 0))
+        load_table(1, 0, T)
+        deal_table_scales(1)
+        load_w1(0, 1, stage("w1_raw", [P, PACK * PASS], F32, 5 * T - 128)[:], 2)
+        w1_raw[1] = stage("w1_raw", [P, 15 * M], F32, first_at + 4 * T - 64)
+        load_w1(1, 0, w1_raw[1][:, M : 5 * M], 1)
+        load_w1(1, 1, w1_raw[1][:, 6 * M : 10 * M], 1)
+        tone_sb = stage("tone_sb", [P, 2, 2 * PACK], F32, first_at + 2 * T)
+        gain_sb = stage("gain_sb", [P, 2, 2 * PACK], F32, first_at + 2 * T + 64)
+        skip_sb = stage("skip_sb", [P, H // P], F32, first_at + 2 * T + 128)
+        load_factor(tone_sb, tone)
+        load_factor(gain_sb, gain)
+        with nc.allow_non_contiguous_dma(reason="one factor for each partition and row tile"):
+            nc.sync.dma_start(skip_sb[:], skip.rearrange("(c q) -> q c", q=P))
+
         w1_bf, w1_q = {}, {}
         second_rebut = w1_raw[1][:, 10 * M : 14 * M]
         first_rebut = w1_raw[1][:, : 12 * M]
-        w1_bf[1, 0] = w1_raw[1][:, 14 * M :].bitcast(BF16)
-        w1_bf[1, 1] = w1_raw[1][:, 13 * M : 15 * M].bitcast(BF16)
+        w1_bf[1, 0] = w1_raw[1][:, 13 * M : 15 * M].bitcast(BF16)
+        last_tiles = w1_raw[1][:, 13 * M : 14 * M].bitcast(BF16)
         first_quoted = keep.tile([P, 2 * M], F32, name="first_quoted", align_bytes=64)
 
         def w1_views(a, g, c0):
@@ -263,9 +257,9 @@ def tile_list_citation_chain_reader_kernel(
             rows = out[a * PASS : (a + 1) * PASS, :].rearrange("(p t) m -> p t m", t=PACK)
             nc.sync.dma_start(rows[:, t, m0 : m0 + mc], rebut[a, 0][:, t, m0 : m0 + mc])
 
-        def fetch_residual(a, tag, parts):
+        def fetch_residual(a, offset, parts):
             rows = out[a * PASS : (a + 1) * PASS, :].rearrange("(c q) m -> q c m", q=P)
-            residual[a] = keep.tile([P, PACK, M], F32, name="residual", tag=tag, align_bytes=64)
+            residual[a] = stage("residual", [P, PACK, M], F32, offset)
             step = M // parts
             for c in range(0, M, step):
                 nc.sync.dma_start(residual[a][:, :, c : c + step], rows[:, :, c : c + step])
@@ -307,10 +301,8 @@ def tile_list_citation_chain_reader_kernel(
                 factor, ALU.mult,
             )
 
-        gather_table(0)
-        nc.vector.tensor_copy(v_sc[:], tab_sc[:].indirect(offs_sb[:]))
         round_w1(0, 0, 0)
-        quantise_w1(0, 0, [PASS], "tab_sc")
+        quantise_w1(0, 0, [PASS])
         gather_table(1)
         round_w1(0, 1, 0)
         dst, src = w1_views(0, 1, PASS // 2)
@@ -325,15 +317,35 @@ def tile_list_citation_chain_reader_kernel(
             first_stage_pass(0, PACK - 1, g)
         for t in range(1, PACK):
             fetch_h(0, t)
+        w23_sc = keep.tile([P, 2 * H], U8, name="w23_sc", tag="w1_bf01", align_bytes=64)
+        nc.gpsimd.memset(w23_sc[:].bitcast(I32), 0)
+        for first, rows in ((4, w3_scales), (0, w2_scales)):
+            for r in range(4):
+                nc.sync.dma_start(
+                    w23_sc[first + r : P : 32, :].bitcast(I32).rearrange("q (a n) -> q a n", a=2),
+                    rows[:, r:16:4, :].rearrange("a q n -> q a n").bitcast(I32),
+                )
+        w3_w = keep.tile([P, 2, H], I32, name="w3_w", tag="w1_00_scales", align_bytes=64)
+        nc.sync.dma_start(w3_w[:], w3_words.rearrange("a p n i -> p a (n i)").bitcast(I32))
+        w2_w = keep.tile([P, 2, 2 * H], U8, name="w2_w", tag="w1_00_codes", align_bytes=64)
+        nc.sync.dma_start(w2_w[:].bitcast(I32), w2_words.rearrange("a p n -> p a n").bitcast(I32))
         round_w1_gpsimd(1, 0, 0, P // 4)
-        quantise_w1(1, 0, [PASS])
-        dst, src = w1_views(1, 1, 0)
-        nc.scalar.copy(dst[:, :, :, :2], src[:, :, :, :2])
-        round_w1_gpsimd(1, 1, 2, P // 2)
+        quantise_w1(1, 0, [PASS], "w1_01_codes")
+        src = w1_part[1, 1, 0].rearrange("p j (m t) -> p m j t", t=PACK)
+        first_tiles = keep.tile([P, 2 * PASS], BF16, name="first_tiles", tag="w1_01_scales", align_bytes=64)
+        nc.scalar.copy(first_tiles[:].rearrange("p (t m j) -> p m j t", t=2, j=PACK), src[:, :, :, :2])
+        dst = last_tiles.rearrange("p (t m j) -> p m t j", t=2, j=PACK)
+        src = src[:, :, :, 2:].rearrange("p m j t -> p m t j")
+        for m2 in (0, P // 2):
+            nc.gpsimd.tensor_scalar(dst[:, m2 : m2 + P // 2], src[:, m2 : m2 + P // 2], 1.0, 0.0, ALU.mult, ALU.add)
         quoted[0, 0] = [rows[:, t * M : (t + 1) * M] for rows in (first_quoted, w1_raw[1][:, M:]) for t in range(2)]
         curved[0, 0] = planes_tile("curved", M, "w1_raw0")
         rebut[0, 0] = first_rebut.rearrange("p (t m) -> p t m", t=PACK)[:, :, :M]
-        quantise_w1(1, 1, [PASS])
+        codes = keep.tile([P, PASS], U32, name="w1_11_codes", align_bytes=64)
+        scales = keep.tile([P, PASS], U8, name="w1_11_scales", align_bytes=64)
+        for values, cols in ((first_tiles[:], slice(0, 2 * P)), (last_tiles, slice(2 * P, PASS))):
+            nc.vector.quantize_mx(out=codes[:, cols].bitcast(FP8X4), scales=scales[:, cols], in_=values)
+        w1_q[1, 1] = codes, scales
         for t in range(PACK):
             gather(quoted[0, 0][t], pos1_sb, 0, 0, M, t)
         for t in range(PACK):
@@ -342,8 +354,8 @@ def tile_list_citation_chain_reader_kernel(
         for g in range(2):
             for t in range(PACK):
                 first_stage_pass(1, t, g)
-        fetch_residual(0, "tab_w1", 1)
-        first_gained = w1_bf[1, 1].rearrange("p (t m) -> p t m", t=PACK)
+        fetch_residual(0, 0, 1)
+        first_gained = w1_bf[1, 0].rearrange("p (t m) -> p t m", t=PACK)
         for t in range(PACK):
             gelu(0, 0, t)
             nc.gpsimd.tensor_scalar(
@@ -355,7 +367,7 @@ def tile_list_citation_chain_reader_kernel(
         for m2, me in CHUNKS:
             b_bf[0, m2] = bf16_tile("b_bf", me, "b_lower")
             weave_gpsimd(b_bf[0, m2], rebut[0, 0], m2, m2 + me)
-            quantise_b(0, m2, [me], "w1_10_codes" if m2 == m0 else None)
+            quantise_b(0, m2, [me], "w1_01_codes" if m2 == m0 else None)
             second_stage_passes("b", 0, m2, me, m2)
 
         x_bf[0, 0] = bf16_tile("x_bf", M, "x_bf0")
@@ -376,7 +388,7 @@ def tile_list_citation_chain_reader_kernel(
         for m2, me in CHUNKS:
             gather(rebut[1, 0][:, 3, m2 : m2 + me], pos2_sb, 1, m2, me, 3)
             park(1, 3, m2, me)
-        fetch_residual(1, "tab_w0", 2)
+        fetch_residual(1, first_at, 2)
 
         curved[1, m0] = planes_tile("curved", mc, "curved_a")
         shared = keep.tile([P, 3 * mc], F32, name="shared", align_bytes=64)

@@ -74,9 +74,9 @@ def tile_list_citation_chain_reader_kernel(
 
         load_table(0, 0, T // 4)
         nc.sync.dma_start(offs_sb[:], offs)
+        nc.sync.dma_start(tab_sc[0:P:4, :].bitcast(I32), tab_scales.rearrange("g q n -> (g q) n").bitcast(I32))
         nc.sync.dma_start(pos1_sb[:], pos1)
         nc.sync.dma_start(pos2_sb[:], pos2)
-        nc.sync.dma_start(tab_sc[0:P:4, :].bitcast(I32), tab_scales.rearrange("g q n -> (g q) n").bitcast(I32))
         load_table(0, T // 4, T)
         w1_raw[0] = keep.tile([P, PACK * PASS], F32, name="w1_raw", tag="w1_raw0", align_bytes=64)
         load_w1(0, 0, w1_raw[0][:], 1)
@@ -106,13 +106,17 @@ def tile_list_citation_chain_reader_kernel(
         w1_raw[1] = stage("w1_raw", [P, 15 * M], F32, first_at + 4 * T - 64)
         load_w1(1, 0, w1_raw[1][:, M : 5 * M], 1)
         load_w1(1, 1, w1_raw[1][:, 6 * M : 10 * M], 1)
-        tone_sb = stage("tone_sb", [P, 2, 2 * PACK], F32, first_at + 2 * T)
-        gain_sb = stage("gain_sb", [P, 2, 2 * PACK], F32, first_at + 2 * T + 64)
-        skip_sb = stage("skip_sb", [P, H // P], F32, first_at + 2 * T + 128)
+        tone_sb = stage("tone_sb", [P, 2, 2 * PACK], F32, first_at + 3 * T)
+        gain_sb = stage("gain_sb", [P, 2, 2 * PACK], F32, first_at + 3 * T + 64)
+        skip_sb = stage("skip_sb", [P, H // P], F32, first_at + 3 * T + 128)
         load_factor(tone_sb, tone)
         load_factor(gain_sb, gain)
         with nc.allow_non_contiguous_dma(reason="one factor for each partition and row tile"):
             nc.sync.dma_start(skip_sb[:], skip.rearrange("(c q) -> q c", q=P))
+        w3_w = stage("w3_w", [P, 2, H], I32, first_at)
+        nc.sync.dma_start(w3_w[:], w3_words.rearrange("a p n i -> p a (n i)").bitcast(I32))
+        w2_w = stage("w2_w", [P, 2, 2 * H], U8, first_at + 2 * T)
+        nc.sync.dma_start(w2_w[:].bitcast(I32), w2_words.rearrange("a p n -> p a n").bitcast(I32))
 
         w1_bf, w1_q = {}, {}
         second_rebut = w1_raw[1][:, 10 * M : 14 * M]
@@ -303,6 +307,14 @@ def tile_list_citation_chain_reader_kernel(
 
         round_w1(0, 0, 0)
         quantise_w1(0, 0, [PASS])
+        w23_sc = keep.tile([P, 2 * H], U8, name="w23_sc", tag="w1_bf00", align_bytes=64)
+        nc.gpsimd.memset(w23_sc[:].bitcast(I32), 0)
+        for r in range(4):
+            for first, rows in ((4, w3_scales), (0, w2_scales)):
+                nc.sync.dma_start(
+                    w23_sc[first + r : P : 32, :].bitcast(I32).rearrange("q (a n) -> q a n", a=2),
+                    rows[:, r:16:4, :].rearrange("a q n -> q a n").bitcast(I32),
+                )
         gather_table(1)
         round_w1(0, 1, 0)
         dst, src = w1_views(0, 1, PASS // 2)
@@ -317,18 +329,6 @@ def tile_list_citation_chain_reader_kernel(
             first_stage_pass(0, PACK - 1, g)
         for t in range(1, PACK):
             fetch_h(0, t)
-        w23_sc = keep.tile([P, 2 * H], U8, name="w23_sc", tag="w1_bf01", align_bytes=64)
-        nc.gpsimd.memset(w23_sc[:].bitcast(I32), 0)
-        for first, rows in ((4, w3_scales), (0, w2_scales)):
-            for r in range(4):
-                nc.sync.dma_start(
-                    w23_sc[first + r : P : 32, :].bitcast(I32).rearrange("q (a n) -> q a n", a=2),
-                    rows[:, r:16:4, :].rearrange("a q n -> q a n").bitcast(I32),
-                )
-        w3_w = keep.tile([P, 2, H], I32, name="w3_w", tag="w1_00_scales", align_bytes=64)
-        nc.sync.dma_start(w3_w[:], w3_words.rearrange("a p n i -> p a (n i)").bitcast(I32))
-        w2_w = keep.tile([P, 2, 2 * H], U8, name="w2_w", tag="w1_00_codes", align_bytes=64)
-        nc.sync.dma_start(w2_w[:].bitcast(I32), w2_words.rearrange("a p n -> p a n").bitcast(I32))
         round_w1_gpsimd(1, 0, 0, P // 4)
         quantise_w1(1, 0, [PASS], "w1_01_codes")
         src = w1_part[1, 1, 0].rearrange("p j (m t) -> p m j t", t=PACK)
@@ -388,7 +388,7 @@ def tile_list_citation_chain_reader_kernel(
         for m2, me in CHUNKS:
             gather(rebut[1, 0][:, 3, m2 : m2 + me], pos2_sb, 1, m2, me, 3)
             park(1, 3, m2, me)
-        fetch_residual(1, first_at, 2)
+        fetch_residual(1, 5 * T - 128, 2)
 
         curved[1, m0] = planes_tile("curved", mc, "curved_a")
         shared = keep.tile([P, 3 * mc], F32, name="shared", align_bytes=64)

from contextlib import ExitStack

import concourse.mybir as mybir

K, H, T, S, M = 1024, 1024, 4096, 1024, 512
FLOPS = 2 * K * H * S + 2 * 2 * H * H * M

F32 = mybir.dt.float32
BF16 = mybir.dt.bfloat16
I32 = mybir.dt.int32
U32 = mybir.dt.uint32
U16 = mybir.dt.uint16
U8 = mybir.dt.uint8
FP8X4 = mybir.dt.float8_e4m3fn_x4
FP4X4 = mybir.dt.float4_e2m1fn_x4
ACT = mybir.ActivationFunctionType
ALU = mybir.AluOpType

P = 128
PACK = 4
PASS = P * PACK
BANK = 512
LIST_ROWS = 16
CHUNKS = ((0, 256), (256, 256))
H_BANKS = (((0, 1, 2, 3), (4, 5), (6, 7), (4, 5)), ((0, 1), (2, 3), (0, 1), (2, 3)))


def tile_list_citation_chain_reader_kernel(
    tc, tab_words, tab_scales, offs, pos1, pos2, w1, w2_words, w2_scales,
    w3_words, w3_scales, tone, gain, skip, out,
):
    nc = tc.nc
    with ExitStack() as ctx:
        lists = ctx.enter_context(tc.tile_pool(name="lists", bufs=1))
        staged = ctx.enter_context(tc.tile_pool(name="staged", bufs=1))
        keep = ctx.enter_context(tc.tile_pool(name="keep", bufs=1))
        psum = ctx.enter_context(tc.psum_pool(name="psum", bufs=1))

        def bank(number, shape):
            return psum.tile(shape, F32, name="bank", tag="bank%d" % number)

        offs_sb = lists.tile([P, S // LIST_ROWS], U16)
        pos1_sb = lists.tile([P, M // LIST_ROWS], U16)
        pos2_sb = lists.tile([P, M // LIST_ROWS], U16)

        def stage(name, shape, dtype, offset):
            return staged.tile(shape, dtype, name=name, offset=offset, align_bytes=64)

        tab_sc = stage("tab_sc", [P, T], U8, 4 * T - 64)
        nc.vector.memset(tab_sc[:].bitcast(I32), 0)

        warm = keep.tile([P, 8], F32)
        nc.vector.memset(warm[:], 0.0)
        nc.scalar.activation(warm[:], warm[:], ACT.Gelu_apprx_tanh)

        first_at = 5 * T - 128 + 16 * PASS
        tab_w = [stage("tab_w", [P, T], I32, first_at)]
        w1_raw, w1_part = {}, {}

        def load_table(g, c0, c1):
            words = tab_words[g].rearrange("p n i -> p (n i)").bitcast(I32)
            nc.sync.dma_start(tab_w[g][:, c0:c1], words[:, c0:c1])

        def load_w1(a, g, raw, parts):
            width = PASS // parts
            for c0 in range(0, PASS, width):
                part = raw[:, c0 * PACK : (c0 + width) * PACK].rearrange("p (j c) -> p j c", j=PACK)
                rows = w1[g * PASS : (g + 1) * PASS, a * PASS + c0 : a * PASS + c0 + width]
                nc.sync.dma_start(part, rows.rearrange("(p j) c -> p j c", j=PACK))
                w1_part[a, g, c0] = part

        def load_factor(dst, vec):
            nc.sync.dma_start(dst[:, :, :PACK], vec.rearrange("(a p t) -> p a t", a=2, t=PACK))

        load_table(0, 0, T // 4)
        nc.sync.dma_start(offs_sb[:], offs)
        nc.sync.dma_start(tab_sc[0:P:4, :].bitcast(I32), tab_scales.rearrange("g q n -> (g q) n").bitcast(I32))
        nc.sync.dma_start(pos1_sb[:], pos1)
        nc.sync.dma_start(pos2_sb[:], pos2)
        load_table(0, T // 4, T)
        w1_raw[0] = keep.tile([P, PACK * PASS], F32, name="w1_raw", tag="w1_raw0", align_bytes=64)
        load_w1(0, 0, w1_raw[0][:], 1)

        v_w = [keep.tile([P, S], U32, name="v_w%d" % g, align_bytes=64) for g in range(2)]
        v_sc = keep.tile([P, S], U8, align_bytes=64)
        nc.vector.memset(v_sc[:].bitcast(I32), 0)
        v_spread = keep.tile([P, S], U8, align_bytes=64)
        nc.vector.tensor_copy(v_spread[:], tab_sc[:].indirect(offs_sb[:]))

        def deal_table_scales(g):
            for r in range(4):
                nc.sync.dma_start(
                    v_sc[4 * g + r : P : 32, :].bitcast(I32),
                    v_spread[64 * g + 4 * r : 64 * (g + 1) : 16, :].bitcast(I32),
                )

        def gather_table(g):
            nc.vector.tensor_copy(v_w[g][:], tab_w[g][:].bitcast(U32).indirect(offs_sb[:]))

        gather_table(0)
        deal_table_scales(0)
        tab_w.append(stage("tab_w", [P, T], I32, 0))
        load_table(1, 0, T)
        deal_table_scales(1)
        load_w1(0, 1, stage("w1_raw", [P, PACK * PASS], F32, 5 * T - 128)[:], 2)
        w1_raw[1] = stage("w1_raw", [P, 15 * M], F32, first_at + 4 * T - 64)
        load_w1(1, 0, w1_raw[1][:, M : 5 * M], 1)
        load_w1(1, 1, w1_raw[1][:, 6 * M : 10 * M], 1)
        tone_sb = stage("tone_sb", [P, 2, 2 * PACK], F32, first_at + 3 * T)
        gain_sb = stage("gain_sb", [P, 2, 2 * PACK], F32, first_at + 3 * T + 64)
        skip_sb = stage("skip_sb", [P, H // P], F32, first_at + 3 * T + 128)
        load_factor(tone_sb, tone)
        load_factor(gain_sb, gain)
        with nc.allow_non_contiguous_dma(reason="one factor for each partition and row tile"):
            nc.sync.dma_start(skip_sb[:], skip.rearrange("(c q) -> q c", q=P))
        w3_w = stage("w3_w", [P, 2, H], I32, first_at)
        nc.sync.dma_start(w3_w[:], w3_words.rearrange("a p n i -> p a (n i)").bitcast(I32))
        w2_w = stage("w2_w", [P, 2, 2 * H], U8, first_at + 2 * T)
        nc.sync.dma_start(w2_w[:].bitcast(I32), w2_words.rearrange("a p n -> p a n").bitcast(I32))

        w1_bf, w1_q = {}, {}
        second_rebut = w1_raw[1][:, 10 * M : 14 * M]
        first_rebut = w1_raw[1][:, : 12 * M]
        w1_bf[1, 0] = w1_raw[1][:, 13 * M : 15 * M].bitcast(BF16)
        last_tiles = w1_raw[1][:, 13 * M : 14 * M].bitcast(BF16)
        first_quoted = keep.tile([P, 2 * M], F32, name="first_quoted", align_bytes=64)

        def w1_views(a, g, c0):
            if (a, g) not in w1_bf:
                w1_bf[a, g] = keep.tile([P, PASS * PACK], BF16, name="w1_bf", tag="w1_bf%d%d" % (a, g), align_bytes=64)
            src = w1_part[a, g, c0].rearrange("p j (m t) -> p m j t", t=PACK)
            dst = w1_bf[a, g][:].rearrange("p (t m j) -> p m j t", t=PACK, j=PACK)
            return dst[:, c0 // PACK : c0 // PACK + src.shape[1]], src

        def round_w1(a, g, c0):
            nc.scalar.copy(*w1_views(a, g, c0))

        def round_w1_gpsimd(a, g, t0, step):
            dst, src = (view[:, :, :, t0:].rearrange("p m j t -> p m t j") for view in w1_views(a, g, 0))
            for m2 in range(0, P, step):
                nc.gpsimd.tensor_scalar(dst[:, m2 : m2 + step], src[:, m2 : m2 + step], 1.0, 0.0, ALU.mult, ALU.add)

        def quantise(name, values, widths, tag=None):
            words = values.shape[1] // PACK
            codes = keep.tile([P, words], U32, name=name + "_codes", tag=tag or name + "_codes", align_bytes=64)
            scales = keep.tile([P, words], U8, name=name + "_scales", align_bytes=64)
            c0 = 0
            for width in widths:
                nc.vector.quantize_mx(
                    out=codes[:, c0 : c0 + width].bitcast(FP8X4),
                    scales=scales[:, c0 : c0 + width],
                    in_=values[:, PACK * c0 : PACK * (c0 + width)],
                )
                c0 += width
            return codes, scales

        def quantise_w1(a, g, widths, tag=None):
            w1_q[a, g] = quantise("w1_%d%d" % (a, g), w1_bf[a, g], widths, tag)

        h_acc, h = {}, {}

        def first_stage_pass(a, t, g):
            codes, scales = w1_q[a, g]
            banks = H_BANKS[a][t]
            width = S // len(banks)
            for half, number in enumerate(banks):
                if g == 0:
                    h_acc[a, t, half] = bank(number, [P, width])
                cols = slice(half * width, (half + 1) * width)
                nc.tensor.matmul_mx(
                    out=h_acc[a, t, half][:],
                    lhsT=codes[:, t * P : (t + 1) * P].bitcast(FP8X4),
                    lhsT_scale=scales[:, t * P : (t + 1) * P],
                    rhs=v_w[g][:, cols].bitcast(FP8X4),
                    rhs_scale=v_sc[4 * g : P, cols],
                    start=(g == 0),
                    stop=(g == 1),
                )

        def fetch_h(a, t, vector_helps=False):
            rows = keep.tile([P, S], F32, name="h", tag="h%d%d" % (a, t), align_bytes=64)
            width = S // len(H_BANKS[a][t])
            for half in range(len(H_BANKS[a][t])):
                if vector_helps and half % 2:
                    nc.vector.tensor_copy(rows[:, half * width : (half + 1) * width], h_acc[a, t, half][:])
                else:
                    nc.scalar.copy(rows[:, half * width : (half + 1) * width], h_acc[a, t, half][:])
            h[a, t] = rows

        quoted, curved, rebut, x_bf, b_bf, x_q, b_q = {}, {}, {}, {}, {}, {}, {}

        def planes_tile(name, mc, tag):
            return keep.tile([P, PACK, mc], F32, name=name, tag=tag, align_bytes=64)

        def gather(dst, picks_sb, a, m0, mc, t):
            picks = picks_sb[:, m0 // LIST_ROWS : (m0 + mc) // LIST_ROWS]
            nc.vector.tensor_copy(dst, h[a, t][:].indirect(picks))

        def gelu(a, m0, t):
            nc.scalar.activation(
                curved[a, m0][:, t, :], quoted[a, m0][t], ACT.Gelu_apprx_tanh, scale=tone_sb[:, a, t : t + 1]
            )

        def woven(tile):
            return tile[:].rearrange("p (c i t) -> p c t i", i=4, t=PACK)

        def planes(tile):
            return tile[:].rearrange("p t (c i) -> p c t i", i=4)

        def bf16_tile(name, mc, tag):
            return keep.tile([P, mc * PACK], BF16, name=name, tag=tag, align_bytes=64)

        def weave(dst, src, c0, c1):
            into = dst.rearrange("p (c i t) -> p c t i", i=4, t=PACK)
            nc.scalar.copy(into, src[:, :, c0:c1].rearrange("p t (c i) -> p c t i", i=4))

        def weave_gpsimd(dst, src, c0, c1):
            for c in range(c0, c1, P):
                nc.gpsimd.tensor_scalar(
                    dst[:, PACK * (c - c0) : PACK * (c - c0 + P)].rearrange("p (m t) -> p m t", t=PACK),
                    src[:, :, c : c + P].rearrange("p t m -> p m t"),
                    1.0, 0.0, ALU.mult, ALU.add,
                )

        def quantise_x(a, m0, widths, tag=None):
            x_q[a, m0] = quantise("x%d_%d" % (a, m0), x_bf[a, m0], widths, tag)

        def quantise_b(a, m0, widths, tag=None):
            b_q[a, m0] = quantise("b%d_%d" % (a, m0), b_bf[a, m0], widths, tag)

        y_acc = {}

        def second_stage_passes(kind, a, m0, mc, piece_m0, last=False):
            codes, scales = (x_q if kind == "x" else b_q)[a, piece_m0]
            cols = slice(m0 - piece_m0, m0 - piece_m0 + mc)
            for c in range(H // P):
                pair, side = divmod(c, 2)
                first = (m0, pair) not in y_acc
                if first:
                    y_acc[m0, pair] = bank(PACK * (m0 // mc) + pair, [P, 2, mc])
                n0 = a * H + c * P
                if kind == "x":
                    weights = w2_w[:, a, 2 * c * P : 2 * (c + 1) * P].bitcast(FP4X4)
                    weight_scales = w23_sc[:, n0 : n0 + P]
                else:
                    weights = w3_w[:, a, c * P : (c + 1) * P].bitcast(FP8X4)
                    weight_scales = w23_sc[4:P, n0 : n0 + P]
                nc.tensor.matmul_mx(
                    out=y_acc[m0, pair][:, side, :],
                    lhsT=weights,
                    lhsT_scale=weight_scales,
                    rhs=codes[:, cols].bitcast(FP8X4),
                    rhs_scale=scales[:, cols],
                    start=first,
                    stop=(last and side == 1),
                )

        residual = {}

        def park(a, t, m0, mc):
            rows = out[a * PASS : (a + 1) * PASS, :].rearrange("(p t) m -> p t m", t=PACK)
            nc.sync.dma_start(rows[:, t, m0 : m0 + mc], rebut[a, 0][:, t, m0 : m0 + mc])

        def fetch_residual(a, offset, parts):
            rows = out[a * PASS : (a + 1) * PASS, :].rearrange("(c q) m -> q c m", q=P)
            residual[a] = stage("residual", [P, PACK, M], F32, offset)
            step = M // parts
            for c in range(0, M, step):
                nc.sync.dma_start(residual[a][:, :, c : c + step], rows[:, :, c : c + step])

        bent, result = {}, {}

        def bend(m0, mc, pair):
            if pair not in bent:
                bent[pair] = keep.tile([P, 2, M], F32, name="bent", tag="bent%d" % pair, align_bytes=64)
            nc.scalar.activation(bent[pair][:, :, m0 : m0 + mc], y_acc[m0, pair][:], ACT.Tanh)

        def finish(m0, mc, pair, singly):
            cols = slice(m0, m0 + mc)
            if m0 == 0:
                result[m0, pair] = keep.tile([P, 2, mc], F32, name="result", tag="result%d" % pair, align_bytes=64)[:]
            else:
                result[m0, pair] = bent[(pair + 2) % PACK][:, :, :mc]
            for side in range(2):
                c = 2 * pair + side
                nc.vector.scalar_tensor_tensor(
                    result[m0, pair][:, side, :], residual[c // PACK][:, c % PACK, cols], skip_sb[:, c : c + 1],
                    bent[pair][:, side, cols], ALU.mult, ALU.add,
                )
                if singly:
                    nc.sync.dma_start(out[c * P : (c + 1) * P, cols], result[m0, pair][:, side, :])
            if not singly:
                rows = out[2 * pair * P : 2 * (pair + 1) * P, cols]
                nc.sync.dma_start(rows.rearrange("(c q) m -> q c m", q=P), result[m0, pair])

        def apply_gain(dst, a, m0, t, c0, c1):
            nc.scalar.activation(dst[:, t, :], curved[a, m0][:, t, c0:c1], ACT.Copy, scale=gain_sb[:, a, t : t + 1])

        def round_x(a, m0, mc, tag):
            x_bf[a, m0] = bf16_tile("x_bf", mc, tag)
            factor = gain_sb[:, a, :PACK].unsqueeze(1).unsqueeze(3).to_broadcast([P, mc // 4, PACK, 4])
            nc.vector.tensor_tensor(
                x_bf[a, m0][:].rearrange("p (c i t) -> p c t i", i=4, t=PACK),
                curved[a, m0][:].rearrange("p t (c i) -> p c t i", i=4),
                factor, ALU.mult,
            )

        round_w1(0, 0, 0)
        quantise_w1(0, 0, [PASS])
        w23_sc = keep.tile([P, 2 * H], U8, name="w23_sc", tag="w1_bf00", align_bytes=64)
        nc.gpsimd.memset(w23_sc[:].bitcast(I32), 0)
        for r in range(4):
            for first, rows in ((4, w3_scales), (0, w2_scales)):
                nc.sync.dma_start(
                    w23_sc[first + r : P : 32, :].bitcast(I32).rearrange("q (a n) -> q a n", a=2),
                    rows[:, r:16:4, :].rearrange("a q n -> q a n").bitcast(I32),
                )
        gather_table(1)
        round_w1(0, 1, 0)
        dst, src = w1_views(0, 1, PASS // 2)
        nc.vector.tensor_copy(dst[:, :, :, 0], src[:, :, :, 0])
        nc.scalar.copy(dst[:, :, :, 1:], src[:, :, :, 1:])
        quantise_w1(0, 1, [P] * PACK)
        for g in range(2):
            for t in range(PACK - 1):
                first_stage_pass(0, t, g)
        fetch_h(0, 0, vector_helps=True)
        for g in range(2):
            first_stage_pass(0, PACK - 1, g)
        for t in range(1, PACK):
            fetch_h(0, t)
        round_w1_gpsimd(1, 0, 0, P // 4)
        quantise_w1(1, 0, [PASS], "w1_01_codes")
        src = w1_part[1, 1, 0].rearrange("p j (m t) -> p m j t", t=PACK)
        first_tiles = keep.tile([P, 2 * PASS], BF16, name="first_tiles", tag="w1_01_scales", align_bytes=64)
        nc.scalar.copy(first_tiles[:].rearrange("p (t m j) -> p m j t", t=2, j=PACK), src[:, :, :, :2])
        dst = last_tiles.rearrange("p (t m j) -> p m t j", t=2, j=PACK)
        src = src[:, :, :, 2:].rearrange("p m j t -> p m t j")
        for m2 in (0, P // 2):
            nc.gpsimd.tensor_scalar(dst[:, m2 : m2 + P // 2], src[:, m2 : m2 + P // 2], 1.0, 0.0, ALU.mult, ALU.add)
        quoted[0, 0] = [rows[:, t * M : (t + 1) * M] for rows in (first_quoted, w1_raw[1][:, M:]) for t in range(2)]
        curved[0, 0] = planes_tile("curved", M, "w1_raw0")
        rebut[0, 0] = first_rebut.rearrange("p (t m) -> p t m", t=PACK)[:, :, :M]
        codes = keep.tile([P, PASS], U32, name="w1_11_codes", align_bytes=64)
        scales = keep.tile([P, PASS], U8, name="w1_11_scales", align_bytes=64)
        for values, cols in ((first_tiles[:], slice(0, 2 * P)), (last_tiles, slice(2 * P, PASS))):
            nc.vector.quantize_mx(out=codes[:, cols].bitcast(FP8X4), scales=scales[:, cols], in_=values)
        w1_q[1, 1] = codes, scales
        for t in range(PACK):
            gather(quoted[0, 0][t], pos1_sb, 0, 0, M, t)
        for t in range(PACK):
            gather(rebut[0, 0][:, t, :], pos2_sb, 0, 0, M, t)
            park(0, t, 0, M)
        for g in range(2):
            for t in range(PACK):
                first_stage_pass(1, t, g)
        fetch_residual(0, 0, 1)
        first_gained = w1_bf[1, 0].rearrange("p (t m) -> p t m", t=PACK)
        for t in range(PACK):
            gelu(0, 0, t)
            nc.gpsimd.tensor_scalar(
                first_gained[:, t, :], curved[0, 0][:, t, :], gain_sb[:, 0, t : t + 1], 0.0, ALU.mult, ALU.add
            )
        for t in range(PACK):
            fetch_h(1, t)
        (m0, mc), (m1, md) = CHUNKS
        for m2, me in CHUNKS:
            b_bf[0, m2] = bf16_tile("b_bf", me, "b_lower")
            weave_gpsimd(b_bf[0, m2], rebut[0, 0], m2, m2 + me)
            quantise_b(0, m2, [me], "w1_01_codes" if m2 == m0 else None)
            second_stage_passes("b", 0, m2, me, m2)

        x_bf[0, 0] = bf16_tile("x_bf", M, "x_bf0")
        weave(x_bf[0, 0][:], first_gained, 0, M)
        quantise_x(0, 0, [M])
        for m2, me in CHUNKS:
            second_stage_passes("x", 0, m2, me, 0)


        quoted_a = planes_tile("quoted", mc, "quoted_a")
        quoted[1, m0] = [quoted_a[:, t, :] for t in range(PACK)]
        rebut[1, 0] = second_rebut.rearrange("p (t m) -> p t m", t=PACK)
        for t in range(PACK - 1):
            gather(rebut[1, 0][:, t, :], pos2_sb, 1, 0, M, t)
            gather(quoted[1, m0][t], pos1_sb, 1, m0, mc, t)
            park(1, t, 0, M)
        gather(quoted[1, m0][3], pos1_sb, 1, m0, mc, 3)
        for m2, me in CHUNKS:
            gather(rebut[1, 0][:, 3, m2 : m2 + me], pos2_sb, 1, m2, me, 3)
            park(1, 3, m2, me)
        fetch_residual(1, 5 * T - 128, 2)

        curved[1, m0] = planes_tile("curved", mc, "curved_a")
        shared = keep.tile([P, 3 * mc], F32, name="shared", align_bytes=64)
        gained = shared[:].bitcast(BF16)[:, 2 * mc :].rearrange("p (t m) -> p t m", t=PACK)
        for t in range(PACK):
            gelu(1, m0, t)
            apply_gain(gained, 1, m0, t, 0, mc)
        x_bf[1, m0] = bf16_tile("x_bf", mc, "x_bf_a")
        weave(x_bf[1, m0][:], gained, 0, mc)
        quantise_x(1, m0, [mc])
        second_stage_passes("x", 1, m0, mc, m0)
        b_bf[1, m0] = bf16_tile("b_bf", mc, "w1_11_codes")
        weave_gpsimd(b_bf[1, m0], rebut[1, 0], m0, m0 + mc)
        b_bf[1, m1] = shared[:, : 2 * mc].bitcast(BF16)
        weave(b_bf[1, m1], rebut[1, 0], m1, m1 + md)

        early = keep.tile([P, PACK - 1, md], F32, name="quoted", tag="curved_a", align_bytes=64)
        quoted[1, m1] = [early[:, 0, :], early[:, 1, :], early[:, 2, :], shared[:, 2 * mc :]]
        curved[1, m1] = planes_tile("curved", md, "curved_b")
        for t in range(PACK):
            gather(quoted[1, m1][t], pos1_sb, 1, m1, md, t)
            gelu(1, m1, t)
        quantise_b(1, m0, [mc], "x_bf_a")
        second_stage_passes("b", 1, m0, mc, m0, last=True)
        quantise_b(1, m1, [md])
        second_stage_passes("b", 1, m1, md, m1)
        round_x(1, m1, md, "x_bf_b")
        quantise_x(1, m1, [md])
        second_stage_passes("x", 1, m1, md, m1, last=True)
        for m2, me in CHUNKS:
            for pair in range(PACK):
                bend(m2, me, pair)
        for m2, me in CHUNKS:
            for pair in range(PACK):
                finish(m2, me, pair, m2 == m1 and pair == PACK - 1)
